import numpy as np, ml_dtypes
CORES = [35,38,43,46]
N = 4
import mx_ref
BF = ml_dtypes.bfloat16
def entries(a):
    return np.ascontiguousarray(a.T).reshape(-1)
def table(e):
    return np.ascontiguousarray(np.reshape(e, (-1, 16)).T).astype(np.int32)
def gentries(a):
    return np.ascontiguousarray(a.reshape(8, 16, -1).transpose(0, 2, 1)).reshape(8, -1)
def gtable(e):
    e = np.asarray(e); return np.ascontiguousarray(e.reshape(8, -1, 16).transpose(0, 2, 1)).reshape(128, -1).astype(np.int32)
def gcols(t, e):
    v = np.concatenate([t.reshape(8, 16, -1, 4), np.zeros((8, 16, 1, 4), BF)], axis=2)
    return np.ascontiguousarray(np.stack([v[g][:, e[g]] for g in range(8)])).reshape(128, -1)
def tile(rs):
    return np.stack(rs, axis=2).reshape(128, -1).astype(BF)
def pick(q, e):
    c = np.concatenate([q[0].reshape(128, -1, 4), np.zeros((128, 1, 4), np.uint8)], axis=1); s = np.concatenate([q[1], np.ones((16, 1), np.uint8)], axis=1)
    return (np.ascontiguousarray(c[:, e].reshape(128, -1)), np.ascontiguousarray(s[:, e]))
def join(*qs):
    return (np.concatenate([q[0] for q in qs], axis=1), np.concatenate([q[1] for q in qs], axis=1))
def put(q, e, v):
    c, s = q[0].reshape(128, -1, 4).copy(), q[1].copy(); c[:, e] = v[0].reshape(128, -1, 4); s[:, e] = v[1]
    return (c.reshape(128, -1), s)
def pk(c, s):
    return (np.ascontiguousarray(c), mx_ref.live(s))
def emit(q):
    return q[0], q[1]
def packed(v, rng):
    q = [mx_ref.quantize(np.ascontiguousarray(v[r])) for r in range(N)]
    return np.stack([a for a, b in q]), np.stack([mx_ref.plane(b, rng) for a, b in q])
def values_of_codes():
    e, c = np.zeros((128, 128, 4), np.float32), np.zeros((128, 2, 4), np.uint8)
    e[np.arange(128), np.arange(128), 0] = 1
    c[:127, :, 0] = np.arange(256).reshape(2, 128).T[:127]
    return mx_ref.matmul(mx_ref.quantize(e.reshape(128, 512).astype(BF)), (c.reshape(128, 8), np.full((16, 2), 127, np.uint8))).T.reshape(-1).astype(np.float64)
CODE_VALUE, SCALE_VALUE = values_of_codes(), 2.0 ** (np.arange(256) - 127.0)
def decode(q):
    return (CODE_VALUE[q[0]].reshape(16, 8, -1, 4) * SCALE_VALUE[q[1]][:, None, :, None] + 0.0).reshape(128, -1).astype(np.float32)
def f(rng, *shape):
    return mx_ref.flush((rng.standard_normal(shape, dtype=np.float32) * np.exp2(rng.integers(-2, 3, shape[:-1] + (1,)))).astype(BF))
def wide(rng, *shape, cols=0):
    v = rng.standard_normal(shape, dtype=np.float32) * np.exp2(rng.integers(-12, 13, shape)).astype(np.float32)
    if cols: v *= np.repeat(np.exp2(rng.integers(-cols, cols + 1, shape[:-2] + (1, shape[-1] // 4))) * (rng.random(shape[:-2] + (1, shape[-1] // 4)) > 0.0625), 4, axis=-1).astype(np.float32)
    return mx_ref.flush(v.astype(BF))
C = 448
STEP = [1, 2, 3]
def numbers_of(rng):
    return {"x": np.array(f(rng, N, 128, 4 * C)), "u": np.array(f(rng, N, 128, 512)), "v": np.array(f(rng, N, 128, 512))}
def orders(rng):
    return rng.permuted(np.tile(np.arange(C), (N, 1)), axis=1)
def pairing(rng):
    p = rng.permuted(np.tile(np.arange(C), (N, 8, 1)), axis=2)
    m = np.zeros((N, 8, C), np.int64)
    np.put_along_axis(m, p[:, :, ::2], p[:, :, 1::2], axis=2)
    np.put_along_axis(m, p[:, :, 1::2], p[:, :, ::2], axis=2)
    return m
def stored(a, t, m):
    return {"la": np.stack([table(a[r]) for r in range(N)]), "lb": np.stack([table(t[r]) for r in range(N)]), "mt": np.stack([gtable(m[r]) for r in range(N)])}
def lists(rng):
    return stored(orders(rng), orders(rng), pairing(rng))
def layers(rng, still=[]):
    w = np.array(f(rng, N, 128, 2048)).reshape(N, 8, 16, 4, 8, 16, 4)
    for i in still:
        w[:, :, i] = 0
        w[:, :, :, :, :, i] = 0
    return w
def weights(rng, w):
    c, p = packed(np.ascontiguousarray(w).reshape(N, 128, 2048), rng)
    return {"wc": c, "ws": p}
def setup_inputs(rng):
    return {**numbers_of(rng), **lists(rng), **weights(rng, layers(rng))}
def setup_inputs_ties(rng):
    d = numbers_of(rng)
    m = pairing(rng)
    o = rng.permutation(N)
    k = rng.integers(0, 4, (N, 8, C))
    k[o[1]] += 1
    k[o[2]] = (np.arange(C) > m[o[2]]) == (rng.permutation(8) < 4)[:, None]
    k[o[3]] = 1
    h = rng.permutation(8)
    k[o[3], h[:4], C - 1] = 2
    k[o[3], h[4:], 0] = 0
    x = d["x"].reshape(N, 8, 16, C, 4)
    x[:, :, 0] = 0
    x[:, :, 0, :, 0] = k.astype(np.float32).astype(BF)
    a = np.tile(np.exp2(rng.integers(-3, 4, (1, 8, 1)).astype(np.float32)), (N, 1, C))
    x[:, :, 8:] = 0
    x[:, :, 8, :, 0] = (-1.125 * a).astype(BF)
    x[:, :, 10, :, 0] = (-0.0703125 * a).astype(BF)
    u = d["u"].reshape(N, 128, 128, 4)
    u[:, :, ::16] = 0
    for r in range(N):
        for i in range(0, 128, 16): u[r, i, i, 0] = 0.0 if r == o[0] else -1.0 if r == o[1] else 1.0
    w = layers(rng, [0])
    w[:, :, :, :, :, 8:] = 0
    for g in range(8):
        w[:, g, 8, 0, g, 8, 0] = -28.0
        for b in range(4): w[:, g, 10, b, g, 9, 0] = -2.0 ** (b - 5)
    return {"x": x.reshape(N, 128, 4 * C), "u": u.reshape(N, 128, 512), "v": d["v"], **stored(orders(rng), orders(rng), m), **weights(rng, w)}
def setup_inputs_near(rng):
    d = numbers_of(rng)
    o = np.zeros(N, np.int64)
    for n, r in enumerate(rng.permutation([r for r in range(N) if r < r ^ STEP[0]])):
        e = rng.integers(2)
        o[r], o[r ^ STEP[0]] = n % 2 * 2 + e, n % 2 * 2 + 1 - e
    x = d["x"].astype(np.float32).reshape(N, 8, 16, C, 4)
    x[:, :, 0] = 0
    x[:, :, 8:] = 0
    u = d["u"].reshape(N, 128, 128, 4)
    u[:, :, ::16] = 0
    w = layers(rng, [0, 1, 8, 9, 10, 11, 12, 13, 14, 15])
    for r in range(N):
        c = rng.choice([-1.0, 1.0], (8, 1))
        s = rng.integers(0, 16, (8, C))
        digits = ((s[:, :, None] >> np.arange(4)) & 1) * np.exp2(np.arange(4) - 23.0)
        if o[r] < 2:
            x[r, :, 0, :, 0] = c
            x[r, :, 8] = digits
            x[r, :, 11, :, 0] = 2.0 ** -10
        elif o[r] == 2:
            x[r, :, 8] = digits * rng.choice([-1.0, 1.0], (8, C, 1))
            x[r, :, 1:8] = 0
            x[r, :, 1, :, 0] = rng.choice([-1.0, 1.0], (8, C)) * 2.0 ** -30
            for g in range(8):
                w[r, g, 1, 0, g, 12, 0] = 2.0 ** -8
                w[r, g, 1, 0, g, 13, 0] = 64.0
        else:
            x[r, :, 8, :, 0] = np.where(s < 8, 1.25, 0.0) * 2.0 ** -30 * c
            x[r, :, 9, :, 0] = np.where(s < 8, 0.0, 1.125) * 2.0 ** -30 * c
            for g in rng.permutation(8)[:4]:
                e = rng.choice([-1.0, 1.0], C) * 2.0 ** -30
                x[r, g, 8, :, 0] = 1.25 * e
                x[r, g, 9, :, 0] = -1.125 * e
        at = [0, C - 1, int(rng.integers(C)), int(rng.integers(C))]
        for g, j in zip(rng.permutation(8)[:4], at): x[r, g, 0, j, 0] = 2.0 ** 29 * rng.choice([-1.0, 1.0])
        k = 1.0 if o[r] == 0 else 2.0 ** -30
        for h in range(0, 128, 16):
            u[r, h, h, 0] = k
            if o[r] < 2: u[r, h + 11, h, 0] = k
            if o[r] < 3: u[r, h + 8, h] = k
            else:
                u[r, h + 8, h, 0] = k
                u[r, h + 9, h, 0] = 1.125 * k
                u[r, h + 12, h, 0] = k
    return {"x": x.reshape(N, 128, 4 * C).astype(BF), "u": u.reshape(N, 128, 512), "v": d["v"], **lists(rng), **weights(rng, w)}
def setup_inputs_odd(rng):
    d = numbers_of(rng)
    x = (1.0 + (2 * rng.integers(0, 64, (N, 16, 8, C, 4)) + 1) * 2.0 ** -7) * np.exp2(-rng.integers(0, 7, (N, 16, 8, C, 4)).astype(np.float64)) * rng.choice([-1.0, 1.0], (N, 16, 8, C, 4))
    x[:, :, 0, :, 0] = 1.96875 * 2.0 ** 8 * rng.choice([-1.0, 1.0], (N, 16, C))
    u = d["u"].reshape(N, 16, 8, 128, 4)
    u[:, :, 0, ::16] = 0
    for r in range(N):
        for n, g in enumerate(rng.permutation(8)[:4]):
            x[r, 2 * g, 1, :, 0] = (8 + rng.integers(0, 2, C)) * 2.0 ** (n % 2 - 8)
            u[r, :, :, 16 * g] = 0
            u[r, 2 * g, 1, 16 * g, 0] = 1.0
    return {"x": x.astype(np.float32).reshape(N, 128, 4 * C).astype(BF), "u": u.reshape(N, 128, 512), "v": d["v"], **lists(rng), **weights(rng, layers(rng, [0, 8]))}
def setup_inputs_ends(rng):
    d = numbers_of(rng)
    o, e = rng.permutation(N) % 4, rng.permutation(N) % 4
    x = np.zeros((N, 8, 16, C, 4))
    u = d["u"].astype(np.float32).reshape(N, 128, 128, 4)
    v = np.zeros((N, 128, 512))
    w = np.zeros((N, 128, 4, 128, 4), np.float32)
    still = int(rng.integers(8))
    i = np.arange(128)
    for r in range(N):
        h = rng.permutation(8)
        c = np.where(h < 2, 0.0, h % 2 * 2.0 - 1.0)[None, :, None]
        large = (0.88 + 0.04 * rng.random((8, 16, C, 4))) * 2.0 ** 30
        if o[r] == 0: x[r] = -large
        if o[r] == 1: x[r] = large * rng.choice([-1.0, 1.0], (C, 1))
        if o[r] == 2: x[r] = -(1.0 + 0.125 * rng.integers(0, 8, (8, 16, C, 4))) * 2.0 ** -30
        if o[r] == 3: x[r] = d["x"][r].astype(np.float32).reshape(8, 16, C, 4)[:, :, :1]
        if o[r] < 2: u[r, :, ::16] = c * (0.9 + 0.1 * rng.random((128, 8, 4))) * 2.0 ** 30
        if o[r] == 2: u[r, :, ::16] = c * (1.0 + 0.125 * rng.integers(0, 8, (128, 8, 4))) * 2.0 ** -30
        if o[r] == 3: u[r, :, ::16] *= np.abs(c).astype(np.float32)
        v[r] = rng.choice([-1.0, 1.0], (128, 512)) * (2.0 ** 30 if o[r] < 2 else 2.0 ** -30)
        k = np.array([0.125, 0.25, 0.5])[rng.permutation(8) % 3]
        if o[r] == 2: k[:] = 32.0
        if o[r] == 3: k[k == 0.125] = 2.0 ** -8
        k[still] = 256.0 if o[r] == 2 else 0.0
        for b in range(4): w[r, i, b, i, b] = k[i // 16]
    a, t, m = orders(rng), orders(rng), pairing(rng)
    j = np.arange(C)
    a[e == 0] = j
    t[e == 0] = j
    m[e == 0] = j ^ 1
    a[e == 1] = C - 1 - j
    t[e == 1] = C - 1 - j
    m[e == 1] = C - 1 - j
    a[e == 2] = (j + 1) % C
    t[e == 2] = (j + C - 1) % C
    m[e == 2] = (j + C // 2) % C
    return {"x": x.astype(np.float32).reshape(N, 128, 4 * C).astype(BF), "u": u.reshape(N, 128, 512).astype(BF), "v": v.astype(np.float32).astype(BF), **stored(a, t, m), **weights(rng, w.astype(BF))}
def setup_inputs_spread(rng):
    d = setup_inputs(rng)
    d["x"] = wide(rng, N, 128, 4 * C, cols=6)
    return d
def check_inputs(d):
    b = []
    for k in ("x", "u", "v"):
        a = np.abs(d[k].astype(np.float32))
        if not (np.isfinite(a).all() and ((a == 0) | (a >= 2.0 ** -30) & (a <= 2.0 ** 30)).all()): b.append("a value of " + k)
    none, least, most = [emit(mx_ref.quantize(np.full((128, 16), k, np.float32).astype(BF)))[1][0, 0] for k in (0.0, 2.0 ** -8, 2.0 ** 8)]
    for r in range(N):
        for k in ("la", "lb"):
            if (np.sort(entries(d[k][r])) != np.arange(C)).any(): b.append(k + ": not every number once")
        m = gentries(d["mt"][r])
        if not ((m >= 0) & (m < C)).all(): b.append("an entry of mt")
        elif (np.take_along_axis(m, m, axis=1) != np.arange(C)).any() or (m == np.arange(C)).any(): b.append("mt: not in pairs")
        if ((d["wc"][r] == 0x7F) | (d["wc"][r] == 0xFF)).any(): b.append("wc: a code that is no number")
        s = mx_ref.live(d["ws"][r])
        if ((s != none) & ((s < least) | (s > most))).any(): b.append("ws: a scale out of range")
        if (((d["wc"][r].reshape(16, 8, 512, 4) & 0x7F) != 0) & (s == none)[:, None, :, None]).any(): b.append("wc: a code other than zero under the scale of zeros")
    return b
def reference(x, u, v, la, lb, mt, wc, ws):
    qu = [mx_ref.quantize(u[r]) for r in range(N)]
    lay = [pk(wc[r], ws[r]) for r in range(N)]
    mate = [gentries(mt[r]) for r in range(N)]
    kept = [[entries(la[r]), entries(lb[r])] for r in range(N)]
    now = [x[r] for r in range(N)]
    here = np.tile(np.arange(C), (8, 1))
    ll = np.zeros((N, 8, C), np.float32)
    for step in STEP:
        went, sent = [], []
        for r in range(N):
            s = mx_ref.matmul(qu[r], mx_ref.quantize(now[r]))[::16] + np.float32(0.0)
            t = np.take_along_axis(s, mate[r], axis=1)
            crossed = np.where(here < mate[r], s < t, t < s)
            e = np.where(crossed, mate[r], here)
            a = [kept[r][0][e[0]], kept[r][1][e[7]]]
            kept[r] = a[:2]
            for g in range(1, 7):
                k = e[g][a[g]]
                a.append(a[g - 1][k[k]])
            went.append(np.stack(a))
            ll[r] = went[r]
            z = mx_ref.quantize(gcols(now[r], went[r]))
            sent.append(mx_ref.quantize(tile([mx_ref.matmul(pick(lay[r], np.arange(128 * b, 128 * b + 128)), z) * np.float32(0.03125) for b in range(4)])))
        made = []
        for r in range(N):
            far = gcols(decode(sent[r ^ step]).astype(BF), went[r][::-1])
            made.append((now[r].astype(np.float32) + far.astype(np.float32)).astype(BF))
        now = made
    y = np.zeros((N, 128, C), np.float32)
    oc, osc = np.zeros((N, 128, 4 * C), np.uint8), np.zeros((N, 16, C), np.uint8)
    for r in range(N):
        q = mx_ref.quantize(now[r])
        y[r] = mx_ref.matmul(mx_ref.quantize(v[r]), q)
        oc[r], osc[r] = emit(q)
    return {"y": y, "ll": ll, "oc": oc, "osc": osc}

@@ -1,0 +1,532 @@
+import math
+from concourse.bass import DstId, RemoteDMATransfer
+from concourse.mybir import dt, AluOpType, ActivationFunctionType
+
+C, RW = 448, 480
+ADD, SUB, MUL, MIN, MAX = AluOpType.add, AluOpType.subtract, AluOpType.mult, AluOpType.min, AluOpType.max
+LT, GT, GE_, EQ, NE = AluOpType.is_lt, AluOpType.is_gt, AluOpType.is_ge, AluOpType.is_equal, AluOpType.not_equal
+AND, SHR = AluOpType.bitwise_and, AluOpType.arith_shift_right
+COPY, IDENT = ActivationFunctionType.Copy, ActivationFunctionType.Identity
+STEP = [1, 2, 3]
+K = {"w1": 10, "ka": 29, "kv": 29, "w45": 14, "g1": [14, 14, 14, 14, 14], "g2": [16, 16, 16, 16, 14], "mt": 14,
+     "hp": [(0, 0), (0, 1), (1, 0), (1, 1)], "z": [[14, 14, 0, 0], [14, 8, 0, 0]], "hg": [[14, 14, 10, 0], [14, 6, 0, 0]]}
+SLOT_E = [1, 2, 7, 0, 4, 6, 4]
+SLOT_D = [1, 3, 7, 7, 5, 5, 4]
+R_M12, R_F34, R_P2, R_P3, R_F56, R_P4, R_P5, R_WOWN, R_GL, R_P1 = 1, 2, 3, 4, 5, 6, 7, 8, 9, 10
+
+SCRATCH = {
+    "X": ("sbuf", [128, 1792], "bfloat16"), "UT": ("sbuf", [128, 512], "bfloat16"), "VT": ("sbuf", [128, 512], "bfloat16"),
+    "XQ": ("sbuf", [128, 448], "float8_e4m3fn_x4"), "XS": ("sbuf", [128, 448], "uint8"),
+    "UQ": ("sbuf", [128, 128], "float8_e4m3fn_x4"), "US": ("sbuf", [128, 128], "uint8"),
+    "URQ": ("sbuf", [128, 128], "float8_e4m3fn_x4"), "URS": ("sbuf", [128, 128], "uint8"),
+    "VQ": ("sbuf", [128, 128], "float8_e4m3fn_x4"), "VS": ("sbuf", [128, 128], "uint8"),
+    "WQ": ("sbuf", [128, 512], "float8_e4m3fn_x4"), "WS": ("sbuf", [128, 512], "uint8"),
+    "BCT": ("sbuf", [128, 512], "bfloat16"), "BCQ": ("sbuf", [128, 128], "float8_e4m3fn_x4"), "BCS": ("sbuf", [128, 128], "uint8"),
+    "ON": ("sbuf", [128, 512], "bfloat16"), "EBT": ("sbuf", [128, 2048], "bfloat16"),
+    "EBQ": ("sbuf", [128, 512], "float8_e4m3fn_x4"), "EBS": ("sbuf", [128, 512], "uint8"),
+    "PS": ("psum", [128, 4096], "float32"),
+    "MTI": ("sbuf", [128, 28], "int32"), "MI": ("sbuf", [128, 288], "int32"), "MO": ("sbuf", [128, 28], "uint16"),
+    "IN": ("sbuf", [128, 480], "float32"), "IN2": ("sbuf", [128, 448], "float32"), "R2": ("sbuf", [128, 448], "float32"), "II": ("sbuf", [128, 480], "bfloat16"),
+    "MW": ("sbuf", [128, 448], "float32"), "SG": ("sbuf", [128, 672], "float32"),
+    "PI": ("sbuf", [128, 1], "int32"), "PC": ("sbuf", [128, 8], "int32"), "PF": ("sbuf", [128, 8], "float32"), "CB": ("sbuf", [128, 24], "float32"),
+    "GE": ("sbuf", [128, 28], "float32"), "DG": ("sbuf", [128, 28], "float32"),
+    "GI": ("sbuf", [128, 28], "int32"), "G1": ("sbuf", [128, 28], "int32"), "G2": ("sbuf", [128, 28], "float32"),
+    "GC": ("sbuf", [128, 28], "float32"), "GV": ("sbuf", [128, 28], "float32"),
+    "GY": ("sbuf", [128, 28], "float32"), "GU": ("sbuf", [128, 28], "float32"), "ZBI": ("sbuf", [128, 28], "float32"),
+    "PL": ("sbuf", [128, 28], "uint16"), "URI": ("sbuf", [128, 8], "int32"), "UO": ("sbuf", [128, 8], "uint16"),
+    "DGI": ("sbuf", [128, 16], "int32"), "DG2": ("sbuf", [128, 16], "int32"), "MD": ("sbuf", [128, 464], "bfloat16"), "MD16": ("sbuf", [128, 16], "bfloat16"),
+    "MK1": ("sbuf", [128, 464], "bfloat16"), "MK2": ("sbuf", [128, 464], "bfloat16"), "RST": ("sbuf", [128, 464], "bfloat16"),
+    "CCI": ("sbuf", [128, 224], "float32"), "CC": ("sbuf", [128, 224], "float32"),
+    "WRI": ("sbuf", [128, 32], "float32"), "WRO": ("sbuf", [128, 32], "uint16"), "WRQ": ("sbuf", [128, 512], "float8_e4m3fn_x4"), "WRS": ("sbuf", [128, 512], "uint8"), "CCB": ("sbuf", [128, 224], "float32"), "DEL": ("sbuf", [128, 224], "float32"),
+    "R": ("sbuf", [128, 448], "float32"), "DD": ("sbuf", [128, 448], "bfloat16"), "TD": ("sbuf", [128, 464], "bfloat16"),
+    "MT": ("sbuf", [128, 896], "bfloat16"), "MQ": ("sbuf", [128, 224], "float8_e4m3fn_x4"), "MS": ("sbuf", [128, 224], "uint8"),
+    "E1": ("sbuf", [128, 224], "float32"), "E2": ("sbuf", [128, 224], "float32"), "OE": ("sbuf", [128, 224], "uint16"),
+    "ZT": ("sbuf", [128, 480], "bfloat16"), "BIG": ("sbuf", [128, RW * 11], "bfloat16"),
+    "W1": ("sbuf", [128, 480], "bfloat16"), "KA": ("sbuf", [128, 480], "bfloat16"), "W23": ("sbuf", [128, 480], "bfloat16"),
+    "MA": ("sbuf", [128, 480], "bfloat16"), "W45": ("sbuf", [128, 480], "bfloat16"), "W6": ("sbuf", [128, 480], "bfloat16"),
+    "WAB0": ("sbuf", [128, 528], "bfloat16"), "WAB1": ("sbuf", [128, 528], "bfloat16"),
+    "KV": ("sbuf", [128, 512], "bfloat16"), "TT1": ("sbuf", [128, 480], "bfloat16"), "TT2": ("sbuf", [128, 480], "bfloat16"), "TT3": ("sbuf", [128, 480], "bfloat16"),
+    "OAB": ("sbuf", [128, 30], "uint16"), "OB": ("sbuf", [128, 30], "uint16"), "OA": ("sbuf", [128, 30], "uint16"),
+    "OK3B": ("sbuf", [128, 30], "uint16"), "OF": ("sbuf", [128, 30], "uint16"),
+    "L7M": ("sbuf", [128, 464], "bfloat16"), "SC1": ("sbuf", [128, 464], "bfloat16"), "SC2": ("sbuf", [128, 464], "bfloat16"),
+    "U5": ("sbuf", [128, 28], "float32"), "U6": ("sbuf", [128, 28], "float32"), "F": ("sbuf", [128, 28], "float32"),
+    "ZO": ("sbuf", [128, 112], "uint16"), "LLO": ("sbuf", [128, 28], "uint16"),
+    "Z": ("sbuf", [128, 1792], "bfloat16"), "ZQ": ("sbuf", [128, 448], "float8_e4m3fn_x4"), "ZS": ("sbuf", [128, 448], "uint8"),
+    "HP": ("sbuf", [128, 1792], "bfloat16"), "HG": ("sbuf", [128, 1792], "bfloat16"),
+    "LW": ("sbuf", [128, 448], "float32"), "YF": ("sbuf", [128, 448], "float32"),
+}
+for _n in range(1, 6):
+    SCRATCH["OK%d" % _n] = ("sbuf", [128, 30], "uint16")
+for _n in range(3):
+    SCRATCH["HQ%d" % _n] = ("sbuf", [128, 448], "float8_e4m3fn_x4")
+    SCRATCH["HS%d" % _n] = ("sbuf", [128, 448], "uint8")
+    SCRATCH["LQ%d" % _n] = ("sbuf", [128, 448], "float8_e4m3fn_x4")
+    SCRATCH["LS%d" % _n] = ("sbuf", [128, 448], "uint8")
+    SCRATCH["LST%d" % _n] = ("sbuf", [128, 28], "uint16")
+    SCRATCH["RL%d" % _n] = ("sbuf", [128, 28], "uint16")
+SEMAPHORES = ["qV", "qS", "qP", "qG", "dx0", "dx1", "du", "dm", "dt1", "dt2", "dw", "dv", "dk", "dmix", "dwb", "dwd", "dwe", "dwf", "dk2", "dk3", "dk4", "drev", "dout", "lsend"]
+SEMAPHORES += ["aL%d" % _n for _n in range(3)] + ["aC%d%d" % (_n, _h) for _n in range(3) for _h in range(2)]
+PSUM_BANK = 512
+
+
+def rank_program(g, core, T, topo):
+    rank = T.rank_of(core)
+    if rank is None:
+        return
+    Q = {"V": g.vector, "S": g.scalar, "P": g.tensor, "G": g, "Y": g.sync}
+    known = {q: {} for q in Q}
+    count, log = {}, {}
+
+    def view(name, c0, c1, step=1, p0=0, p1=128):
+        return (name, c0, c1, step, p0, p1)
+
+    def ap(v):
+        n, c0, c1, step, p0, p1 = v
+        return T[n][p0:p1, c0:c1] if step == 1 else T[n][p0:p1, c0:c1:step]
+
+    def access(v, w):
+        n, c0, c1, step, p0, p1 = v
+        if n == "PS":
+            return (n, c0 // PSUM_BANK, (c1 - 1) // PSUM_BANK + 1, 1, 0, 128, True)
+        return (n, c0, c1, step, p0, p1, w)
+
+    def hit(a, b):
+        if a[4] >= b[5] or b[4] >= a[5] or a[1] >= b[2] or b[1] >= a[2]:
+            return False
+        k = math.gcd(a[3], b[3])
+        return k == 1 or (a[1] - b[1]) % k == 0
+
+    def issue(q, fn, reads, writes, sem=None, inc=16, chain=True):
+        accs = [(access(v, False), False) for v in reads] + [(access(v, True), True) for v in writes]
+        need = []
+        for a, w in accs:
+            for (b, bw, bq, tok) in log.get(a[0], []):
+                if not (a[6] or b[6]) or not hit(a, b):
+                    continue
+                if bq == q and sem is None and not bw:
+                    continue
+                s, n, snap = tok
+                if bq == "dma":
+                    n = count[s]
+                need.append((s, n, snap))
+        need.sort(key=lambda e: -len(e[2]))
+        for s, n, snap in sorted(need, key=lambda e: (-e[1] if e[0] in ("qV", "qS", "qP", "qG") else 0)):
+            if known[q].get(s, 0) >= n:
+                continue
+            Q[q].wait_ge(T.sem[s], int(n))
+            for k2, v2 in snap.items():
+                known[q][k2] = max(known[q].get(k2, 0), v2)
+            known[q][s] = n
+        inst = fn()
+        name = sem if sem is not None else "q" + q
+        count[name] = count.get(name, 0) + (inc if sem is not None else 1)
+        if chain:
+            inst.then_inc(T.sem[name], inc if sem is not None else 1)
+        tok = (name, count[name], dict(known[q]))
+        for a, w in accs:
+            lst = log.setdefault(a[0], [])
+            if w or a[0] == "PS":
+                if a[3] == 1:
+                    lst[:] = [e for e in lst if not (a[1] <= e[0][1] and e[0][2] <= a[2] and a[4] <= e[0][4] and e[0][5] <= a[5])]
+            else:
+                lst[:] = [e for e in lst if not (e[0] == a and e[2] == q and q != "Y" and sem is None and not e[1])]
+            lst.append((a, w, "dma" if sem is not None else q, tok))
+
+    def sc(v):
+        return ap(v) if isinstance(v, tuple) else v
+
+    def src(a):
+        if len(a) == 2:
+            return ap(a[0]).indirect(ap(a[1])), [a[0], a[1]]
+        return ap(a), [a]
+
+    def ts(out, in0, s1, s2=None, op0=ADD, op1=None):
+        e, rd = src(in0)
+        rd = rd + [s for s in (s1, s2) if isinstance(s, tuple)]
+        if op1 is None:
+            issue("V", lambda: g.vector.tensor_scalar(ap(out), e, sc(s1), None, op0), rd, [out])
+        else:
+            issue("V", lambda: g.vector.tensor_scalar(ap(out), e, sc(s1), sc(s2), op0, op1), rd, [out])
+
+    def tt(out, in0, in1, op):
+        e, rd = src(in0)
+        issue("V", lambda: g.vector.tensor_tensor(ap(out), e, ap(in1), op), rd + [in1], [out])
+
+    def cp(q, out, in_):
+        e, rd = src(in_)
+        if q == "V":
+            issue("V", lambda: g.vector.tensor_copy(ap(out), e), rd, [out])
+        else:
+            issue("S", lambda: g.scalar.activation(ap(out), e, COPY), rd, [out])
+
+    def fill(out, k):
+        issue("V", lambda: g.vector.memset(ap(out), k), [], [out])
+
+    def turn(out, in_):
+        issue("V", lambda: g.vector.transpose(ap(out), ap(in_)), [in_], [out])
+
+    def quant(q, s, c0, c1, t, e0):
+        o, p, i = view(q, c0, c1), view(s, c0, c1), view(t, e0, e0 + 4 * (c1 - c0))
+        issue("V", lambda: g.vector.quantize_mx(ap(o), ap(p), ap(i)), [i], [o, p])
+
+    def mm(bank, n, wq, ws, w0, xq, xs, x0):
+        o = view("PS", PSUM_BANK * bank, PSUM_BANK * bank + n)
+        a, b, c, d = view(wq, w0, w0 + 128), view(ws, w0, w0 + 128), view(xq, x0, x0 + n), view(xs, x0, x0 + n)
+        issue("P", lambda: g.tensor.matmul_mx(ap(o), ap(a), ap(b), ap(c), ap(d), True, True), [a, b, c, d], [o])
+
+    def dma(q, out, in_, sem, oap=None, iap=None):
+        o = oap if oap is not None else ap(out)
+        i = iap if iap is not None else ap(in_)
+        issue(q, lambda: Q[q].dma_start(o, i), [in_] if in_ is not None else [], [out] if out is not None else [], sem=sem)
+
+    def send(dst, oname, iname, c0, c1, rsem, codes):
+        rid, pid, _s = topo.addr(dst)
+        i, o = T[iname][:, c0:c1], T[oname][:, c0:c1]
+        if codes:
+            i, o = i.bitcast(dt.uint8), o.bitcast(dt.uint8)
+        n = len(topo.engines(core, dst))
+        issue("G", lambda: g.remote_dma(o, i, T.sem[rsem], T.sem["lsend"], pid, rid, topo.mask(core, dst)), [view(iname, c0, c1)], [], sem="lsend", inc=n, chain=False)
+
+    def arrives(name, c0, c1, sem, n):
+        count[sem] = count.get(sem, 0) + n
+        log.setdefault(name, []).append((access(view(name, c0, c1), True), True, "dma", (sem, count[sem], {})))
+
+    def iota(out, pattern, base, ch, flag):
+        if flag:
+            issue("G", lambda: g.iota(ap(out), pattern, base, ch, allow_small_or_imprecise_dtypes=True), [], [out])
+        else:
+            issue("G", lambda: g.iota(ap(out), pattern, base, ch), [], [out])
+
+    def pf(k):
+        return view("PF", k, k + 1)
+
+    def cb(k):
+        return view("CB", k, k + 1)
+
+    def region(r, a=0, b=464):
+        return view("BIG", RW * r + a, RW * r + b)
+
+    def two(r):
+        return view("BIG", RW * r, RW * (r + 2))
+
+    def gather(q, out, win, off):
+        cp(q, view(out[0], out[1], out[1] + 464), (win, view(off[0], off[1], off[1] + 29)))
+
+    def split(out, win, off, k=16):
+        if k < 29:
+            cp("S", view(out[0], out[1] + 16 * k, out[1] + 464), (win, view(off[0], off[1] + k, off[1] + 29)))
+        if k > 0:
+            cp("V", view(out[0], out[1], out[1] + 16 * k), (win, view(off[0], off[1], off[1] + k)))
+
+    def planes(out, h, b, win, off, o0, k):
+        o = o0 + 14 * h
+        if k > 0:
+            cp("V", view(out, 896 * h + b, 896 * h + 64 * k, 4), (win, view(off, o, o + k)))
+        if k < 14:
+            cp("S", view(out, 896 * h + 64 * k + b, 896 * h + 896, 4), (win, view(off, o + k, o + 14)))
+
+    fill(view("MI", 0, 288), 0)
+    dma("Y", view("MTI", 0, 28), None, "dm", iap=T.mt[:, :])
+    dma("Y", view("X", 0, 896), None, "dx0", iap=T.x[:, 0:896])
+    dma("S", view("X", 896, 1792), None, "dx1", iap=T.x[:, 896:1792])
+    dma("Y", view("UT", 0, 512), None, "du", iap=T.u[:, :])
+    k = 0
+    for s in range(7):
+        for par in range(2):
+            gr = (SLOT_E, SLOT_D)[par][s]
+            a = 32 * s + 1 - par
+            dma("YS"[k % 2], view("MI", a, a + 28, 1, 16 * par, 16 * par + 16), None, "dt1", iap=T.mt[16 * gr:16 * gr + 16, :])
+            k += 1
+    for s, par, t in ((7, 0, T.la), (7, 1, T.lb), (8, 0, T.lb), (8, 1, T.lb)):
+        a = 32 * s + 1 - par
+        dma("YS"[k % 2], view("MI", a, a + 28, 1, 16 * par, 16 * par + 16), None, "dt1", iap=t[:, :])
+        k += 1
+    for b in range(1, 4):
+        dma("Y", view("MI", 0, 288, 1, 32 * b, 32 * b + 32), view("MI", 0, 288, 1, 0, 32), "dt2")
+    dma("Y", view("WQ", 0, 512), None, "dw", oap=T.WQ[:, 0:512].bitcast(dt.uint8), iap=T.wc[:, :])
+    dma("Y", view("WS", 0, 512), None, "dw", iap=T.ws[:, :])
+    dma("Y", view("VT", 0, 512), None, "dv", iap=T.v[:, :])
+
+    iota(view("PI", 0, 1), [[0, 1]], 0, 1, False)
+    iota(view("DGI", 0, 16), [[1, 16]], 128, -1, False)
+    iota(view("URI", 0, 8), [[16, 8]], 0, 0, False)
+    iota(view("IN", 0, 480), [[1, 480]], 0, 0, True)
+    iota(view("ZT", 0, 480), [[0, 480]], 0, 0, True)
+    iota(view("ZBI", 0, 28), [[0, 7], [128, 4]], 0, 0, True)
+
+    iota(view("CCI", 0, 224), [[0, 7], [16, 32]], 0, 0, True)
+
+    iota(view("WRI", 0, 32), [[128, 4], [-16, 8]], 112, 0, True)
+    iota(view("ON", 0, 512), [[0, 512]], 1, 0, True)
+    cp("S", view("IN2", 0, 448), view("IN", 0, 448))
+    cp("S", view("BCT", 0, 480), view("ZT", 0, 480))
+    cp("S", view("BCT", 480, 512), view("ZT", 0, 32))
+    cp("S", view("MT", 0, 448), view("ZT", 0, 448))
+    cp("S", view("MT", 448, 896), view("ZT", 0, 448))
+    on = view("ON", 0, 512)
+
+    def pick(out, in_, pattern, op, fill_, base, ch):
+        issue("G", lambda: g.affine_select(ap(out), ap(in_), pattern, op, fill_, base, ch), [in_], [out])
+    pick(view("RST", 0, 464), view("ON", 0, 464), [[0, 29], [1, 16]], NE, 0.0, 0, 0)
+    for h in range(8):
+        pick(view("MD", 0, 464), view("MD" if h else "ZT", 0, 464), [[0, 29], [-1, 16]], NE, 1.0, -16 * h, 1)
+    issue("G", lambda: g.affine_select(ap(on), ap(on), [[16, 8], [-1, 16], [0, 4]], EQ, 0.0, -112, 1), [on], [on])
+    for b in range(4):
+        o = view("EBT", 512 * b, 512 * b + 512)
+        issue("G", lambda o=o, b=b: g.affine_select(ap(o), ap(on), [[0, 128], [1, 4]], EQ, 0.0, -b, 0), [on], [o])
+
+    p = view("PI", 0, 1)
+    for k, m in ((0, 16), (1, 31), (2, 15), (4, 3), (6, 1)):
+        ts(view("PC", k, k + 1), p, m, None, AND)
+    ts(view("PC", 3, 4), p, 4, None, SHR)
+    ts(view("PC", 5, 6), p, 2, 3, SHR, AND)
+    cp("V", view("PC", 7, 8), p)
+    for s in range(7):
+        fill(view("GE", 4 * s, 4 * s + 4), float(SLOT_E[s]))
+        fill(view("DG", 4 * s, 4 * s + 4), float(SLOT_D[s] - SLOT_E[s]))
+    cp("V", view("PF", 0, 8), view("PC", 0, 8))
+    ts(view("DG2", 0, 16), view("DGI", 0, 16), 15, None, AND)
+    ts(view("UO", 0, 8), view("URI", 0, 8), 0.0, None, ADD)
+    fill(view("TD", 448, 464), 0.0)
+    ts(view("MD16", 0, 16), view("DG2", 0, 16), 0.0, None, EQ)
+    for h in range(8):
+        cp("S", view("BCT", 64 * h + 2 * (h % 2), 64 * h + 64, 4), view("MD16", 0, 16))
+    for r in (0, R_GL, R_P3, R_P5):
+        cp("S", region(r, 0, 480), view("ZT", 0, 480))
+
+    def full(n):
+        return view(n, 0, 28)
+    ts(cb(5), pf(4), 0.0, None, EQ)
+    ts(cb(6), pf(4), 3.0, None, EQ)
+    ts(cb(9), pf(5), 32.0, None, MUL)
+    ts(full("GU"), full("DG"), pf(6), None, MUL)
+    tt(cb(7), cb(5), cb(6), ADD)
+    ts(cb(10), cb(5), -32.0, None, MUL)
+    tt(full("GI"), full("GU"), full("GE"), ADD)
+    tt(cb(8), pf(3), cb(7), SUB)
+    tt(cb(11), cb(9), cb(10), ADD)
+    ts(full("G1"), full("GI"), 1, None, AND)
+    cp("V", full("MO"), full("MTI"))
+    tt(view("MW", 0, 448), (view("IN", 0, 448), full("MO")), view("IN2", 0, 448), SUB)
+    quant("UQ", "US", 0, 128, "UT", 0)
+    ts(view("SG", 0, 448), view("MW", 0, 448), 0.0, 0.5, GT, SUB)
+    ts(view("SG", 448, 672), view("MW", 224, 448), 0.0, 0.5, AluOpType.is_le, SUB)
+    uq, us, uo = view("UQ", 0, 128), view("US", 0, 128), view("UO", 0, 8)
+    issue("V", lambda: g.vector.tensor_copy(T.URQ[:, 0:128].bitcast(dt.uint32), T.UQ[:, 0:128].bitcast(dt.uint32).indirect(T.UO[:, 0:8])), [uq, uo], [view("URQ", 0, 128)])
+    cp("V", view("URS", 0, 128), (us, uo))
+    quant("XQ", "XS", 0, 224, "X", 0)
+    quant("XQ", "XS", 224, 448, "X", 896)
+    tt(full("G2"), full("GI"), full("G1"), SUB)
+    ts(full("GV"), full("G1"), 16.0, cb(11), MUL, ADD)
+    ts(full("GC"), full("G2"), cb(8), None, EQ)
+    tt(full("GV"), full("GV"), full("ZBI"), ADD)
+    ts(full("GY"), full("GV"), 448.0, 448.0, MIN, SUB)
+    ts(full("GU"), full("GV"), 0.0, None, GE_)
+    tt(full("GY"), full("GY"), full("GC"), MUL)
+    tt(full("GU"), full("GY"), full("GU"), MUL)
+    ts(full("PL"), full("GU"), 448.0, None, ADD)
+
+    def tables():
+        ts(cb(2), pf(0), 240.0, None, SUB)
+        ts(cb(3), pf(1), 16.0, None, SUB)
+        ts(cb(4), pf(0), -0.0625, 1.0, MUL, ADD)
+        ts(cb(19), pf(0), -1.0, 16.0, MUL, ADD)
+        ii, n_, c_ = view("II", 0, 480), view("IN", 0, 480), cb(2)
+        issue("S", lambda: g.scalar.activation(ap(ii), ap(n_), IDENT, bias=ap(c_)), [n_, c_], [ii])
+        ts(view("E2", 0, 224), view("CCI", 0, 224), cb(3), None, ADD)
+        wq, wo = view("WQ", 0, 512), view("WRO", 0, 32)
+        ts(wo, view("WRI", 0, 32), pf(2), None, ADD)
+        issue("V", lambda: g.vector.tensor_copy(T.WRQ[:, 0:512].bitcast(dt.uint32), T.WQ[:, 0:512].bitcast(dt.uint32).indirect(T.WRO[:, 0:32])), [wq, wo], [view("WRQ", 0, 512)])
+        ts(view("OAB", 0, 30), view("MI", 224, 254), cb(19), None, ADD)
+        ts(view("OB", 0, 30), view("MI", 256, 286), cb(19), None, ADD)
+        ts(view("CC", 0, 224), view("E2", 0, 224), 0.0, 447.0, MAX, MIN)
+        cp("S", view("WAB0", 16, 480), (view("II", 0, 480), view("OAB", 0, 29)))
+        cp("S", region(R_WOWN, 0, 480), view("ZT", 0, 480))
+        for k in (R_M12, R_F34, R_P2, R_F56, R_P4, R_P1):
+            cp("S", region(k, 464, 480), view("ZT", 0, 16))
+        tt(view("DEL", 0, 224), view("MI", 0, 224), view("CC", 0, 224), SUB)
+        ts(view("CCB", 0, 224), view("CC", 0, 224), cb(19), None, ADD)
+        ts(view("DEL", 192, 224), view("DEL", 192, 224), cb(4), None, MUL)
+        ts(cb(1), pf(0), -31.0, 720.0, MUL, ADD)
+        fill(view("KV", 464, 512), 0.0)
+
+    def late(n):
+        if n == 1:
+            ts(cb(0), pf(0), -1.0, 240.0, MUL, ADD)
+            ts(cb(16), pf(3), 5.0, None, NE)
+            ts(cb(17), pf(0), -1.0, 496.0, MUL, ADD)
+            fill(view("OF", 28, 30), 480)
+            tt(cb(18), cb(17), cb(16), MUL)
+            ts(view("OF", 0, 28), view("CCI", 0, 28), pf(2), cb(18), ADD, ADD)
+        if n == 2:
+            ts(cb(12), pf(7), 96.0, None, GE_)
+            ts(cb(13), pf(7), 112.0, None, GE_)
+            tt(cb(14), cb(12), cb(13), SUB)
+        if n == 4:
+            ts(view("MK1", 0, 464), view("MD", 0, 464), cb(13), None, MAX)
+            ts(view("MK2", 0, 464), view("MD", 0, 464), cb(13), None, MUL)
+            for nm in ("WAB0", "WAB1"):
+                fill(view(nm, 0, 16), 0.0)
+                fill(view(nm, 480, 528), 0.0)
+        if n == 5:
+            cp("S", view("WRS", 0, 512), (view("WS", 0, 512), view("WRO", 0, 32)))
+
+    def offsets(out, te, to, host, base, p0=0, p1=128):
+        ts(view(out, 0, 30, 2, p0, p1), view(te, 16 * host, 480, 32, p0, p1), base, None, ADD)
+        ts(view(out, 1, 30, 2, p0, p1), view(to, 16 * host, 480, 32, p0, p1), base, None, ADD)
+
+    def base_at(k, p0, p1):
+        return view("CB", k, k + 1, 1, p0, p1)
+
+    II = view("II", 0, 480)
+    for r in range(3):
+        peer = T.cores[rank ^ STEP[r]]
+        n_in = len(topo.engines(peer, core))
+        arrives("RL%d" % r, 0, 28, "aL%d" % r, n_in)
+        for h in range(2):
+            count["aC%d%d" % (r, h)] = 2 * n_in
+            for nm in ("LQ%d" % r, "LS%d" % r):
+                log.setdefault(nm, []).append((access(view(nm, 224 * h, 224 * h + 224), True), True, "dma", ("aC%d%d" % (r, h), 2 * n_in, {})))
+        wab, wnew = "WAB%d" % (r % 2), "WAB%d" % ((r + 1) % 2)
+        for h in range(2):
+            mm(h, 224, "URQ", "URS", 0, "XQ", "XS", 224 * h)
+        for h in range(2):
+            tt(view("R", 224 * h, 224 * h + 224), view("PS", 512 * h, 512 * h + 224), view("SG", 224 * h, 224 * h + 224), MUL)
+        r2, rh = view("R2", 0, 224), view("R", 0, 224)
+        issue("S", lambda: g.scalar.activation(ap(r2), ap(rh), COPY, scale=-1.0), [rh], [r2])
+        tt(view("R2", 224, 448), view("PS", 512, 736), view("SG", 448, 672), MUL)
+        tt(view("DD", 0, 448), (view("R", 0, 448), full("MO")), view("R2", 0, 448), LT)
+        turn(view("TD", 0, 448), view("DD", 0, 448))
+        k = K["mt"]
+        cp("S", view("MT", 32 * k, 896, 2), (view("TD", 0, 464), view("PL", k, 28)))
+        cp("V", view("MT", 0, 32 * k, 2), (view("TD", 0, 464), view("PL", 0, k)))
+        if r == 0:
+            quant("BCQ", "BCS", 0, 128, "BCT", 0)
+        quant("MQ", "MS", 0, 224, "MT", 0)
+        mm(2, 224, "BCQ", "BCS", 0, "MQ", "MS", 0)
+        if r == 0:
+            tables()
+        parts = ((0, 64), (64, 224))
+        for a, b in parts:
+            tt(view("E1", a, b), view("PS", 1024 + a, 1024 + b), view("DEL", a, b), MUL)
+        tt(view("E2", 0, 64), view("E1", 0, 64), view("CCB", 0, 64), ADD)
+        cp("V", view("OE", 0, 64), view("E2", 0, 64))
+        tt(view("E2", 64, 224), view("E1", 64, 224), view("CCB", 64, 224), ADD)
+        split(("W1", 0), II, ("OE", 0), K["w1"])
+        gather("S", ("W23", 0), II, ("OE", 32))
+        dma("Y", region(R_WOWN, 0, 464)[:4] + (32, 64), view("W23", 0, 464, 1, 32, 64), "dwd")
+        cp("V", view("OE", 64, 224), view("E2", 64, 224))
+        split(("KA", 0), view("W1", 0, 464), ("OB", 0), K["ka"])
+        gather("S", ("MA", 0), view("W23", 0, 464), ("OAB", 0))
+        split(("KV", 0), view("KA", 0, 464), ("OE", 64), K["kv"])
+        gather("S", ("BIG", RW * R_M12), view("MA", 0, 464), ("OE", 96))
+        turn(view("TT1", 0, 480), view("KV", 0, 480))
+        turn(view("TT2", 0, 480), view("KV", 16, 496))
+        offsets("OK1", "TT1", "TT2", 0, cb(1))
+        w_in = {1: 0, 2: R_M12, 3: R_F34, 4: R_P3, 5: R_F56}
+        w_out = {1: R_P1, 2: R_P2, 3: R_P3, 4: R_P4, 5: R_P5}
+        for n in range(1, 6):
+            ok, host = "OK%d" % n, (n + 1) % 2
+            if n == 1:
+                split(("W45", 0), II, ("OE", 128), K["w45"])
+                dma("Y", region(R_WOWN, 0, 464)[:4] + (64, 80), view("W45", 0, 464, 1, 64, 80), "dwe")
+            split(("BIG", RW * w_out[n]), two(w_in[n]), (ok, 0), K["g1"][n - 1])
+            split(("KV", 16 * host), two(w_out[n] - 1 + host), (ok, 0), K["g2"][n - 1])
+            if n == 1:
+                gather("S", ("BIG", RW * R_F34), view("W45", 0, 464), ("OE", 32))
+            if n == 2:
+                gather("S", ("W6", 0), II, ("OE", 160))
+                dma("Y", region(R_WOWN, 0, 464)[:4] + (96, 112), view("W6", 0, 464, 1, 96, 112), "dwf")
+            if n == 3:
+                gather("S", ("BIG", RW * R_F56), view("W6", 0, 464), ("OE", 192))
+            if n == 4:
+                gather("S", (wnew, 16), view(wab, 16, 496), ("OE", 96))
+            if n == 5:
+                cp("S", region(R_WOWN, 0, 464)[:4] + (0, 32), view(wnew, 16, 480, 1, 0, 32))
+            turn(view("TT1", 0, 480), view("KV", 0, 480))
+            turn(view("TT2", 0, 480), view("KV", 16, 496))
+            if n < 5:
+                offsets("OK%d" % (n + 1), "TT1", "TT2", host, cb(1))
+            else:
+                offsets("OF", "TT1", "TT2", host, base_at(1, 96, 128), 96, 128)
+            if r == 0:
+                late(n)
+            if n == 1:
+                dma("Y", view("OF", 0, 28, 1, 32, 48), view("OK2", 1, 29, 1, 32, 48), "dk2")
+            if n == 2:
+                offsets("OK3B", "TT1", "TT2", host, 704.0)
+                dma("Y", view("OF", 0, 28, 1, 48, 64), view("OK3B", 0, 28, 1, 48, 64), "dk3")
+            if n == 3:
+                dma("Y", view("OF", 0, 28, 1, 64, 80), view("OK4", 1, 29, 1, 64, 80), "dk4")
+        gl = region(R_GL)
+        tt(gl, (two(R_P5), view("OF", 0, 29)), view("MK1", 0, 464), MUL)
+        tt(view("L7M", 0, 464), (two(R_GL), view("OF", 0, 29)), view("MK2", 0, 464), MUL)
+        rst = view("RST", 0, 464)
+
+        def scan(o, i):
+            issue("V", lambda: g.vector.tensor_tensor_scan(ap(o), ap(rst), ap(i), 0.0, MUL, ADD), [rst, i], [o])
+        scan(view("SC1", 0, 464), gl)
+        scan(view("SC2", 0, 464), view("L7M", 0, 464))
+        ts(view("U6", 0, 28, 1, 96, 128), view("SC1", 31, 464, 16, 96, 128), view("CB", 14, 15, 1, 96, 128), None, MUL)
+        cp("V", view("F", 0, 28, 1, 0, 96), view("SC1", 15, 448, 16, 0, 96))
+        tt(view("F", 0, 28, 1, 96, 128), view("SC2", 15, 448, 16, 96, 128), view("U6", 0, 28, 1, 96, 128), ADD)
+        for t in (2, 0, 3, 1):
+            ts(view("ZO", 28 * t, 28 * t + 28), full("F"), 4.0, float(896 + t), MUL, ADD)
+        ts(full("LST%d" % r), full("F"), 224.0, None, ADD)
+        send(peer, "RL%d" % r, "LST%d" % r, 0, 28, "aL%d" % r, False)
+        for h in range(2):
+            for t in range(4):
+                planes("Z", h, t, view("X", 0, 1792), "ZO", 28 * t, K["z"][h][t])
+            quant("ZQ", "ZS", 224 * h, 224 * h + 224, "Z", 896 * h)
+            for b in range(4):
+                mm(4 * h + b, 224, "WRQ", "WRS", 128 * b, "ZQ", "ZS", 224 * h)
+        for h in range(2):
+            for b in range(4):
+                o, i = view("HP", 448 * b + 224 * h, 448 * b + 224 * h + 224), view("PS", 512 * (4 * h + b), 512 * (4 * h + b) + 224)
+                if (h, b) in K["hp"]:
+                    ts(o, i, 0.03125, None, MUL)
+                else:
+                    issue("S", lambda o=o, i=i: g.scalar.activation(ap(o), ap(i), COPY, scale=0.03125), [i], [o])
+        for h in range(2):
+            for b in range(4):
+                planes("HG", h, b, view("HP", 448 * b, 448 * b + 448), "RL%d" % r, 0, K["hg"][h][b])
+            quant("HQ%d" % r, "HS%d" % r, 224 * h, 224 * h + 224, "HG", 896 * h)
+            send(peer, "LQ%d" % r, "HQ%d" % r, 224 * h, 224 * h + 224, "aC%d%d" % (r, h), True)
+            send(peer, "LS%d" % r, "HS%d" % r, 224 * h, 224 * h + 224, "aC%d%d" % (r, h), False)
+        if r < 2:
+            turn(view("TT1", 0, 480), view(wnew, 0, 480))
+            turn(view("TT2", 0, 480), view(wnew, 16, 496))
+            turn(view("TT3", 0, 480), view(wnew, 32, 512))
+            offsets("OB", "TT1", "TT2", 1, cb(0))
+            offsets("OA", "TT2", "TT3", 0, cb(0))
+            offsets("OAB", "TT1", "TT2", 1, cb(0))
+            for k in range(4):
+                dma("Y", view("OAB", 0, 30, 1, 32 * k, 32 * k + 16), view("OA", 0, 30, 1, 32 * k, 32 * k + 16), "dmix")
+        else:
+            ts(full("LLO"), full("F"), cb(0), None, ADD)
+            lw, llo = view("LW", 0, 448), full("LLO")
+            issue("S", lambda: g.scalar.activation(ap(lw), ap(II).indirect(ap(llo)), IDENT, bias=224.0), [II, llo], [lw])
+            dma("Y", None, lw, "dout", oap=T.ll[:, :], iap=T.LW[0:128:16, :])
+            quant("VQ", "VS", 0, 128, "VT", 0)
+        if r == 0:
+            for b in range(4):
+                quant("EBQ", "EBS", 128 * b, 128 * b + 128, "EBT", 512 * b)
+        for h in range(2):
+            for b in range(4):
+                mm(4 * h + b, 224, "EBQ", "EBS", 128 * b, "LQ%d" % r, "LS%d" % r, 224 * h)
+            for b in range(4):
+                x = view("X", 896 * h + b, 896 * h + 896, 4)
+                tt(x, x, view("PS", 512 * (4 * h + b), 512 * (4 * h + b) + 224), ADD)
+            quant("XQ", "XS", 224 * h, 224 * h + 224, "X", 896 * h)
+    for h in range(2):
+        q, s = view("XQ", 224 * h, 224 * h + 224), view("XS", 224 * h, 224 * h + 224)
+        mm(h, 224, "VQ", "VS", 0, "XQ", "XS", 224 * h)
+        dma("Y", None, q, "dout", oap=T.oc[:, 896 * h:896 * h + 896], iap=T.XQ[:, 224 * h:224 * h + 224].bitcast(dt.uint8))
+        for k in range(4):
+            dma("Y", None, s, "dout", oap=T.osc[4 * k:4 * k + 4, 224 * h:224 * h + 224], iap=T.XS[32 * k:32 * k + 4, 224 * h:224 * h + 224])
+        y = view("YF", 224 * h, 224 * h + 224)
+        cp("VS"[h], y, view("PS", 512 * h, 512 * h + 224))
+        dma("Y" if h == 0 else "S", None, y, "dout", oap=T.y[:, 224 * h:224 * h + 224])
+    for s in sorted(count):
+        if known["G"].get(s, 0) < count[s]:
+            g.wait_ge(T.sem[s], int(count[s]))

@@ -1,62 +1,48 @@
 import math
-from concourse.bass import DstId, RemoteDMATransfer
 from concourse.mybir import dt, AluOpType, ActivationFunctionType
 
 C, RW = 448, 480
 ADD, SUB, MUL, MIN, MAX = AluOpType.add, AluOpType.subtract, AluOpType.mult, AluOpType.min, AluOpType.max
 LT, GT, GE_, EQ, NE = AluOpType.is_lt, AluOpType.is_gt, AluOpType.is_ge, AluOpType.is_equal, AluOpType.not_equal
-AND, SHR = AluOpType.bitwise_and, AluOpType.arith_shift_right
+AND = AluOpType.bitwise_and
 COPY, IDENT = ActivationFunctionType.Copy, ActivationFunctionType.Identity
 STEP = [1, 2, 3]
-K = {"w1": 10, "ka": 29, "kv": 29, "w45": 14, "g1": [14, 14, 14, 14, 14], "g2": [16, 16, 16, 16, 14], "mt": 14,
-     "hp": [(0, 0), (0, 1), (1, 0), (1, 1)], "z": [[14, 14, 0, 0], [14, 8, 0, 0]], "hg": [[14, 14, 10, 0], [14, 6, 0, 0]]}
-SLOT_E = [1, 2, 7, 0, 4, 6, 4]
-SLOT_D = [1, 3, 7, 7, 5, 5, 4]
-R_M12, R_F34, R_P2, R_P3, R_F56, R_P4, R_P5, R_WOWN, R_GL, R_P1 = 1, 2, 3, 4, 5, 6, 7, 8, 9, 10
+ROW_A, ROW_B, ROW_L = 0, 7, 8
+R_P = 7
+K = {"g1": 14, "g2": 12, "odd": 14, "even": 8, "last": 12, "cut": [0, 14, 28],
+     "hp": [(0, 0), (0, 1), (1, 0), (1, 1)], "z": [[14, 12, 0, 0], [14, 8, 0, 0]], "hg": [[14, 14, 6, 0], [14, 6, 0, 0]]}
 
 SCRATCH = {
-    "X": ("sbuf", [128, 1792], "bfloat16"), "UT": ("sbuf", [128, 512], "bfloat16"), "VT": ("sbuf", [128, 512], "bfloat16"),
+    "X": ("sbuf", [128, 1792], "bfloat16"), "XP": ("sbuf", [128, 1792], "bfloat16"),
+    "UT": ("sbuf", [128, 512], "bfloat16"), "VT": ("sbuf", [128, 512], "bfloat16"),
     "XQ": ("sbuf", [128, 448], "float8_e4m3fn_x4"), "XS": ("sbuf", [128, 448], "uint8"),
     "UQ": ("sbuf", [128, 128], "float8_e4m3fn_x4"), "US": ("sbuf", [128, 128], "uint8"),
     "URQ": ("sbuf", [128, 128], "float8_e4m3fn_x4"), "URS": ("sbuf", [128, 128], "uint8"),
     "VQ": ("sbuf", [128, 128], "float8_e4m3fn_x4"), "VS": ("sbuf", [128, 128], "uint8"),
     "WQ": ("sbuf", [128, 512], "float8_e4m3fn_x4"), "WS": ("sbuf", [128, 512], "uint8"),
-    "BCT": ("sbuf", [128, 512], "bfloat16"), "BCQ": ("sbuf", [128, 128], "float8_e4m3fn_x4"), "BCS": ("sbuf", [128, 128], "uint8"),
-    "ON": ("sbuf", [128, 512], "bfloat16"), "EBT": ("sbuf", [128, 2048], "bfloat16"),
+    "WRQ": ("sbuf", [128, 512], "float8_e4m3fn_x4"), "WRS": ("sbuf", [128, 512], "uint8"),
+    "WRI": ("sbuf", [128, 32], "float32"), "WRO": ("sbuf", [128, 32], "uint16"),
+    "BCT": ("sbuf", [128, 1024], "bfloat16"), "BCQ": ("sbuf", [128, 256], "float8_e4m3fn_x4"), "BCS": ("sbuf", [128, 256], "uint8"),
+    "ON": ("sbuf", [128, 512], "bfloat16"), "ONE": ("sbuf", [128, 128], "bfloat16"), "EBT": ("sbuf", [128, 2048], "bfloat16"),
     "EBQ": ("sbuf", [128, 512], "float8_e4m3fn_x4"), "EBS": ("sbuf", [128, 512], "uint8"),
     "PS": ("psum", [128, 4096], "float32"),
-    "MTI": ("sbuf", [128, 28], "int32"), "MI": ("sbuf", [128, 288], "int32"), "MO": ("sbuf", [128, 28], "uint16"),
-    "IN": ("sbuf", [128, 480], "float32"), "IN2": ("sbuf", [128, 448], "float32"), "R2": ("sbuf", [128, 448], "float32"), "II": ("sbuf", [128, 480], "bfloat16"),
-    "MW": ("sbuf", [128, 448], "float32"), "SG": ("sbuf", [128, 672], "float32"),
-    "PI": ("sbuf", [128, 1], "int32"), "PC": ("sbuf", [128, 8], "int32"), "PF": ("sbuf", [128, 8], "float32"), "CB": ("sbuf", [128, 24], "float32"),
-    "GE": ("sbuf", [128, 28], "float32"), "DG": ("sbuf", [128, 28], "float32"),
-    "GI": ("sbuf", [128, 28], "int32"), "G1": ("sbuf", [128, 28], "int32"), "G2": ("sbuf", [128, 28], "float32"),
-    "GC": ("sbuf", [128, 28], "float32"), "GV": ("sbuf", [128, 28], "float32"),
-    "GY": ("sbuf", [128, 28], "float32"), "GU": ("sbuf", [128, 28], "float32"), "ZBI": ("sbuf", [128, 28], "float32"),
-    "PL": ("sbuf", [128, 28], "uint16"), "URI": ("sbuf", [128, 8], "int32"), "UO": ("sbuf", [128, 8], "uint16"),
-    "DGI": ("sbuf", [128, 16], "int32"), "DG2": ("sbuf", [128, 16], "int32"), "MD": ("sbuf", [128, 464], "bfloat16"), "MD16": ("sbuf", [128, 16], "bfloat16"),
-    "MK1": ("sbuf", [128, 464], "bfloat16"), "MK2": ("sbuf", [128, 464], "bfloat16"), "RST": ("sbuf", [128, 464], "bfloat16"),
-    "CCI": ("sbuf", [128, 224], "float32"), "CC": ("sbuf", [128, 224], "float32"),
-    "WRI": ("sbuf", [128, 32], "float32"), "WRO": ("sbuf", [128, 32], "uint16"), "WRQ": ("sbuf", [128, 512], "float8_e4m3fn_x4"), "WRS": ("sbuf", [128, 512], "uint8"), "CCB": ("sbuf", [128, 224], "float32"), "DEL": ("sbuf", [128, 224], "float32"),
-    "R": ("sbuf", [128, 448], "float32"), "DD": ("sbuf", [128, 448], "bfloat16"), "TD": ("sbuf", [128, 464], "bfloat16"),
-    "MT": ("sbuf", [128, 896], "bfloat16"), "MQ": ("sbuf", [128, 224], "float8_e4m3fn_x4"), "MS": ("sbuf", [128, 224], "uint8"),
-    "E1": ("sbuf", [128, 224], "float32"), "E2": ("sbuf", [128, 224], "float32"), "OE": ("sbuf", [128, 224], "uint16"),
-    "ZT": ("sbuf", [128, 480], "bfloat16"), "BIG": ("sbuf", [128, RW * 11], "bfloat16"),
-    "W1": ("sbuf", [128, 480], "bfloat16"), "KA": ("sbuf", [128, 480], "bfloat16"), "W23": ("sbuf", [128, 480], "bfloat16"),
-    "MA": ("sbuf", [128, 480], "bfloat16"), "W45": ("sbuf", [128, 480], "bfloat16"), "W6": ("sbuf", [128, 480], "bfloat16"),
-    "WAB0": ("sbuf", [128, 528], "bfloat16"), "WAB1": ("sbuf", [128, 528], "bfloat16"),
-    "KV": ("sbuf", [128, 512], "bfloat16"), "TT1": ("sbuf", [128, 480], "bfloat16"), "TT2": ("sbuf", [128, 480], "bfloat16"), "TT3": ("sbuf", [128, 480], "bfloat16"),
-    "OAB": ("sbuf", [128, 30], "uint16"), "OB": ("sbuf", [128, 30], "uint16"), "OA": ("sbuf", [128, 30], "uint16"),
-    "OK3B": ("sbuf", [128, 30], "uint16"), "OF": ("sbuf", [128, 30], "uint16"),
-    "L7M": ("sbuf", [128, 464], "bfloat16"), "SC1": ("sbuf", [128, 464], "bfloat16"), "SC2": ("sbuf", [128, 464], "bfloat16"),
-    "U5": ("sbuf", [128, 28], "float32"), "U6": ("sbuf", [128, 28], "float32"), "F": ("sbuf", [128, 28], "float32"),
-    "ZO": ("sbuf", [128, 112], "uint16"), "LLO": ("sbuf", [128, 28], "uint16"),
+    "MTI": ("sbuf", [128, 28], "int32"), "MO": ("sbuf", [128, 28], "uint16"), "MO2": ("sbuf", [128, 28], "uint16"),
+    "OLI": ("sbuf", [128, 28], "int32"), "OL": ("sbuf", [128, 28], "uint16"),
+    "IN": ("sbuf", [128, 448], "float32"), "IN2": ("sbuf", [128, 448], "float32"), "SG": ("sbuf", [128, 448], "bfloat16"), "SG0": ("sbuf", [128, 448], "bfloat16"),
+    "AW": ("sbuf", [128, 448], "bfloat16"), "ND": ("sbuf", [128, 896], "float16"), "TAB": ("sbuf", [128, 896], "float16"),
+    "FL": ("sbuf", [128, 896], "bfloat16"), "EW": ("sbuf", [128, 960], "bfloat16"),
+    "PI": ("sbuf", [128, 1], "int32"), "PC": ("sbuf", [128, 4], "int32"), "PF": ("sbuf", [128, 4], "float32"), "CB": ("sbuf", [128, 8], "float32"),
+    "URI": ("sbuf", [128, 8], "int32"), "UO": ("sbuf", [128, 8], "uint16"), "OFI": ("sbuf", [128, 28], "int32"),
+    "R": ("sbuf", [128, 448], "float32"), "R2": ("sbuf", [128, 448], "float32"),
+    "MT": ("sbuf", [128, 1024], "bfloat16"), "MQ": ("sbuf", [128, 256], "float8_e4m3fn_x4"), "MS": ("sbuf", [128, 256], "uint8"),
+    "BIG": ("sbuf", [128, RW * 8], "bfloat16"), "KV": ("sbuf", [128, 448], "bfloat16"),
+    "TT": ("sbuf", [128, 480], "bfloat16"), "TA": ("sbuf", [128, 448], "bfloat16"), "TB": ("sbuf", [128, 480], "bfloat16"),
+    "OA": ("sbuf", [128, 30], "uint16"), "OB": ("sbuf", [128, 30], "uint16"), "OF": ("sbuf", [128, 28], "uint16"),
+    "OK0": ("sbuf", [128, 30], "uint16"), "OK1": ("sbuf", [128, 30], "uint16"),
     "Z": ("sbuf", [128, 1792], "bfloat16"), "ZQ": ("sbuf", [128, 448], "float8_e4m3fn_x4"), "ZS": ("sbuf", [128, 448], "uint8"),
     "HP": ("sbuf", [128, 1792], "bfloat16"), "HG": ("sbuf", [128, 1792], "bfloat16"),
     "LW": ("sbuf", [128, 448], "float32"), "YF": ("sbuf", [128, 448], "float32"),
 }
-for _n in range(1, 6):
-    SCRATCH["OK%d" % _n] = ("sbuf", [128, 30], "uint16")
 for _n in range(3):
     SCRATCH["HQ%d" % _n] = ("sbuf", [128, 448], "float8_e4m3fn_x4")
     SCRATCH["HS%d" % _n] = ("sbuf", [128, 448], "uint8")
@@ -64,8 +50,8 @@ for _n in range(3):
     SCRATCH["LS%d" % _n] = ("sbuf", [128, 448], "uint8")
     SCRATCH["LST%d" % _n] = ("sbuf", [128, 28], "uint16")
     SCRATCH["RL%d" % _n] = ("sbuf", [128, 28], "uint16")
-SEMAPHORES = ["qV", "qS", "qP", "qG", "dx0", "dx1", "du", "dm", "dt1", "dt2", "dw", "dv", "dk", "dmix", "dwb", "dwd", "dwe", "dwf", "dk2", "dk3", "dk4", "drev", "dout", "lsend"]
-SEMAPHORES += ["aL%d" % _n for _n in range(3)] + ["aC%d%d" % (_n, _h) for _n in range(3) for _h in range(2)]
+SEMAPHORES = ["qV", "qS", "qP", "qG", "dx0", "dx1", "du", "dm", "dl", "dw", "dv", "dtab", "dout", "lsend"]
+SEMAPHORES += ["aL%d" % _n for _n in range(3)] + ["aC%d%d" % (_n, _h) for _n in range(3) for _h in range(3)]
 PSUM_BANK = 512
 
 
@@ -96,7 +82,7 @@ def rank_program(g, core, T, topo):
         k = math.gcd(a[3], b[3])
         return k == 1 or (a[1] - b[1]) % k == 0
 
-    def issue(q, fn, reads, writes, sem=None, inc=16, chain=True):
+    def issue(q, fn, reads, writes, sem=None, inc=16, chain=True, rows=False):
         accs = [(access(v, False), False) for v in reads] + [(access(v, True), True) for v in writes]
         need = []
         for a, w in accs:
@@ -106,6 +92,8 @@ def rank_program(g, core, T, topo):
                 if bq == q and sem is None and not bw:
                     continue
                 s, n, snap = tok
+                if rows and s == sem:
+                    continue
                 if bq == "dma":
                     n = count[s]
                 need.append((s, n, snap))
@@ -126,7 +114,7 @@ def rank_program(g, core, T, topo):
         for a, w in accs:
             lst = log.setdefault(a[0], [])
             if w or a[0] == "PS":
-                if a[3] == 1:
+                if a[3] == 1 and not rows:
                     lst[:] = [e for e in lst if not (a[1] <= e[0][1] and e[0][2] <= a[2] and a[4] <= e[0][4] and e[0][5] <= a[5])]
             else:
                 lst[:] = [e for e in lst if not (e[0] == a and e[2] == q and q != "Y" and sem is None and not e[1])]
@@ -159,6 +147,10 @@ def rank_program(g, core, T, topo):
         else:
             issue("S", lambda: g.scalar.activation(ap(out), e, COPY), rd, [out])
 
+    def act(out, in_, scale=1.0, bias=0.0):
+        e, rd = src(in_)
+        issue("S", lambda: g.scalar.activation(ap(out), e, IDENT if bias else COPY, bias=bias, scale=scale), rd, [out])
+
     def fill(out, k):
         issue("V", lambda: g.vector.memset(ap(out), k), [], [out])
 
@@ -169,15 +161,18 @@ def rank_program(g, core, T, topo):
         o, p, i = view(q, c0, c1), view(s, c0, c1), view(t, e0, e0 + 4 * (c1 - c0))
         issue("V", lambda: g.vector.quantize_mx(ap(o), ap(p), ap(i)), [i], [o, p])
 
-    def mm(bank, n, wq, ws, w0, xq, xs, x0):
-        o = view("PS", PSUM_BANK * bank, PSUM_BANK * bank + n)
-        a, b, c, d = view(wq, w0, w0 + 128), view(ws, w0, w0 + 128), view(xq, x0, x0 + n), view(xs, x0, x0 + n)
-        issue("P", lambda: g.tensor.matmul_mx(ap(o), ap(a), ap(b), ap(c), ap(d), True, True), [a, b, c, d], [o])
+    def bank(b, n):
+        return view("PS", PSUM_BANK * b, PSUM_BANK * b + n)
 
-    def dma(q, out, in_, sem, oap=None, iap=None):
+    def mm(b, n, wq, ws, w0, xq, xs, x0):
+        o = bank(b, n)
+        a, e, c, d = view(wq, w0, w0 + 128), view(ws, w0, w0 + 128), view(xq, x0, x0 + n), view(xs, x0, x0 + n)
+        issue("P", lambda: g.tensor.matmul_mx(ap(o), ap(a), ap(e), ap(c), ap(d), True, True), [a, e, c, d], [o])
+
+    def dma(q, out, in_, sem, oap=None, iap=None, rows=False):
         o = oap if oap is not None else ap(out)
         i = iap if iap is not None else ap(in_)
-        issue(q, lambda: Q[q].dma_start(o, i), [in_] if in_ is not None else [], [out] if out is not None else [], sem=sem)
+        issue(q, lambda: Q[q].dma_start(o, i), [in_] if in_ is not None else [], [out] if out is not None else [], sem=sem, rows=rows)
 
     def send(dst, oname, iname, c0, c1, rsem, codes):
         rid, pid, _s = topo.addr(dst)
@@ -187,9 +182,10 @@ def rank_program(g, core, T, topo):
         n = len(topo.engines(core, dst))
         issue("G", lambda: g.remote_dma(o, i, T.sem[rsem], T.sem["lsend"], pid, rid, topo.mask(core, dst)), [view(iname, c0, c1)], [], sem="lsend", inc=n, chain=False)
 
-    def arrives(name, c0, c1, sem, n):
-        count[sem] = count.get(sem, 0) + n
-        log.setdefault(name, []).append((access(view(name, c0, c1), True), True, "dma", (sem, count[sem], {})))
+    def arrives(names, c0, c1, sem, n):
+        count[sem] = n * len(names)
+        for name in names:
+            log.setdefault(name, []).append((access(view(name, c0, c1), True), True, "dma", (sem, count[sem], {})))
 
     def iota(out, pattern, base, ch, flag):
         if flag:
@@ -197,336 +193,227 @@ def rank_program(g, core, T, topo):
         else:
             issue("G", lambda: g.iota(ap(out), pattern, base, ch), [], [out])
 
+    def pick(out, in_, pattern, op, fill_, base, ch):
+        issue("G", lambda: g.affine_select(ap(out), ap(in_), pattern, op, fill_, base, ch), [in_], [out])
+
+    def pick_codes(oq, os_, q, s, n, off, k, sq):
+        o, i, f = view(oq, 0, 16 * k), view(q, 0, n), view(off, 0, k)
+        issue("V", lambda: g.vector.tensor_copy(ap(o).bitcast(dt.uint32), ap(i).bitcast(dt.uint32).indirect(ap(f))), [i, f], [o])
+        cp(sq, view(os_, 0, 16 * k), (view(s, 0, n), f))
+
     def pf(k):
         return view("PF", k, k + 1)
 
     def cb(k):
         return view("CB", k, k + 1)
 
-    def region(r, a=0, b=464):
+    def full(n):
+        return view(n, 0, 28)
+
+    def region(r, a=0, b=RW):
         return view("BIG", RW * r + a, RW * r + b)
 
-    def two(r):
-        return view("BIG", RW * r, RW * (r + 2))
-
-    def gather(q, out, win, off):
-        cp(q, view(out[0], out[1], out[1] + 464), (win, view(off[0], off[1], off[1] + 29)))
-
-    def split(out, win, off, k=16):
-        if k < 29:
-            cp("S", view(out[0], out[1] + 16 * k, out[1] + 464), (win, view(off[0], off[1] + k, off[1] + 29)))
+    def split(out, o0, win, off, k, n=29):
+        if k < n:
+            cp("S", view(out, o0 + 16 * k, o0 + 16 * n), (win, view(off, k, n)))
         if k > 0:
-            cp("V", view(out[0], out[1], out[1] + 16 * k), (win, view(off[0], off[1], off[1] + k)))
+            cp("V", view(out, o0, o0 + 16 * k), (win, view(off, 0, k)))
 
-    def planes(out, h, b, win, off, o0, k):
-        o = o0 + 14 * h
+    def turn2(out, name, c0, n, k):
+        turn(view(out, 0, k), view(name, c0, c0 + k))
+        turn(view(out, k, n), view(name, c0 + k, c0 + n))
+
+    def planes(out, a, e, b, win, off, k):
         if k > 0:
-            cp("V", view(out, 896 * h + b, 896 * h + 64 * k, 4), (win, view(off, o, o + k)))
-        if k < 14:
-            cp("S", view(out, 896 * h + 64 * k + b, 896 * h + 896, 4), (win, view(off, o + k, o + 14)))
+            cp("V", view(out, 64 * a + b, 64 * (a + k), 4), (win, view(off, a, a + k)))
+        if a + k < e:
+            cp("S", view(out, 64 * (a + k) + b, 64 * e, 4), (win, view(off, a + k, e)))
 
-    fill(view("MI", 0, 288), 0)
-    dma("Y", view("MTI", 0, 28), None, "dm", iap=T.mt[:, :])
-    dma("Y", view("X", 0, 896), None, "dx0", iap=T.x[:, 0:896])
+    IN, EW, TAB, ND = view("IN", 0, C), view("EW", 0, 960), view("TAB", 0, 896), view("ND", 0, 896)
+    iota(full("OLI"), [[16, 28]], 0, 1, False)
+    iota(view("PI", 0, 1), [[0, 1]], 0, 1, False)
+    iota(view("URI", 0, 8), [[16, 8]], 0, 0, False)
+    iota(IN, [[1, C]], 0, 0, True)
+    dma("Y", full("MTI"), None, "dm", iap=T.mt[:, :])
     dma("S", view("X", 896, 1792), None, "dx1", iap=T.x[:, 896:1792])
-    dma("Y", view("UT", 0, 512), None, "du", iap=T.u[:, :])
-    k = 0
-    for s in range(7):
-        for par in range(2):
-            gr = (SLOT_E, SLOT_D)[par][s]
-            a = 32 * s + 1 - par
-            dma("YS"[k % 2], view("MI", a, a + 28, 1, 16 * par, 16 * par + 16), None, "dt1", iap=T.mt[16 * gr:16 * gr + 16, :])
-            k += 1
-    for s, par, t in ((7, 0, T.la), (7, 1, T.lb), (8, 0, T.lb), (8, 1, T.lb)):
-        a = 32 * s + 1 - par
-        dma("YS"[k % 2], view("MI", a, a + 28, 1, 16 * par, 16 * par + 16), None, "dt1", iap=t[:, :])
-        k += 1
-    for b in range(1, 4):
-        dma("Y", view("MI", 0, 288, 1, 32 * b, 32 * b + 32), view("MI", 0, 288, 1, 0, 32), "dt2")
+    dma("Y", view("X", 0, 896), None, "dx0", iap=T.x[:, 0:896])
+    dma("S", view("UT", 0, 512), None, "du", iap=T.u[:, :])
+    dma("Y", view("OLI", 0, 28, 1, 0, 16), None, "dl", iap=T.la[:, :])
+    dma("S", view("OLI", 0, 28, 1, 112, 128), None, "dl", iap=T.lb[:, :])
     dma("Y", view("WQ", 0, 512), None, "dw", oap=T.WQ[:, 0:512].bitcast(dt.uint8), iap=T.wc[:, :])
     dma("Y", view("WS", 0, 512), None, "dw", iap=T.ws[:, :])
     dma("Y", view("VT", 0, 512), None, "dv", iap=T.v[:, :])
 
-    iota(view("PI", 0, 1), [[0, 1]], 0, 1, False)
-    iota(view("DGI", 0, 16), [[1, 16]], 128, -1, False)
-    iota(view("URI", 0, 8), [[16, 8]], 0, 0, False)
-    iota(view("IN", 0, 480), [[1, 480]], 0, 0, True)
-    iota(view("ZT", 0, 480), [[0, 480]], 0, 0, True)
-    iota(view("ZBI", 0, 28), [[0, 7], [128, 4]], 0, 0, True)
-
-    iota(view("CCI", 0, 224), [[0, 7], [16, 32]], 0, 0, True)
-
-    iota(view("WRI", 0, 32), [[128, 4], [-16, 8]], 112, 0, True)
-    iota(view("ON", 0, 512), [[0, 512]], 1, 0, True)
-    cp("S", view("IN2", 0, 448), view("IN", 0, 448))
-    cp("S", view("BCT", 0, 480), view("ZT", 0, 480))
-    cp("S", view("BCT", 480, 512), view("ZT", 0, 32))
-    cp("S", view("MT", 0, 448), view("ZT", 0, 448))
-    cp("S", view("MT", 448, 896), view("ZT", 0, 448))
-    on = view("ON", 0, 512)
-
-    def pick(out, in_, pattern, op, fill_, base, ch):
-        issue("G", lambda: g.affine_select(ap(out), ap(in_), pattern, op, fill_, base, ch), [in_], [out])
-    pick(view("RST", 0, 464), view("ON", 0, 464), [[0, 29], [1, 16]], NE, 0.0, 0, 0)
-    for h in range(8):
-        pick(view("MD", 0, 464), view("MD" if h else "ZT", 0, 464), [[0, 29], [-1, 16]], NE, 1.0, -16 * h, 1)
-    issue("G", lambda: g.affine_select(ap(on), ap(on), [[16, 8], [-1, 16], [0, 4]], EQ, 0.0, -112, 1), [on], [on])
-    for b in range(4):
-        o = view("EBT", 512 * b, 512 * b + 512)
-        issue("G", lambda o=o, b=b: g.affine_select(ap(o), ap(on), [[0, 128], [1, 4]], EQ, 0.0, -b, 0), [on], [o])
-
+    fill(view("ONE", 0, 128), 1.0)
+    fill(view("BCT", 0, 1024), 0.0)
     p = view("PI", 0, 1)
-    for k, m in ((0, 16), (1, 31), (2, 15), (4, 3), (6, 1)):
+    for k, m in enumerate((15, 16, 96, 112)):
         ts(view("PC", k, k + 1), p, m, None, AND)
-    ts(view("PC", 3, 4), p, 4, None, SHR)
-    ts(view("PC", 5, 6), p, 2, 3, SHR, AND)
-    cp("V", view("PC", 7, 8), p)
-    for s in range(7):
-        fill(view("GE", 4 * s, 4 * s + 4), float(SLOT_E[s]))
-        fill(view("DG", 4 * s, 4 * s + 4), float(SLOT_D[s] - SLOT_E[s]))
-    cp("V", view("PF", 0, 8), view("PC", 0, 8))
-    ts(view("DG2", 0, 16), view("DGI", 0, 16), 15, None, AND)
+    fill(view("TAB", 0, 896, 2), 0.0)
+    cp("V", view("PF", 0, 4), view("PC", 0, 4))
     ts(view("UO", 0, 8), view("URI", 0, 8), 0.0, None, ADD)
-    fill(view("TD", 448, 464), 0.0)
-    ts(view("MD16", 0, 16), view("DG2", 0, 16), 0.0, None, EQ)
-    for h in range(8):
-        cp("S", view("BCT", 64 * h + 2 * (h % 2), 64 * h + 64, 4), view("MD16", 0, 16))
-    for r in (0, R_GL, R_P3, R_P5):
-        cp("S", region(r, 0, 480), view("ZT", 0, 480))
+    fill(view("FL", 0, 896, 2), 0.0)
+    ts(cb(0), pf(3), 112.0, pf(3), NE, MUL)
+    fill(view("MT", 0, 1024), 0.0)
+    cp("S", view("IN2", 0, C), IN)
+    act(view("TAB", 1, 896, 2), IN, bias=-224.0)
+    for s in range(2):
+        pick(view("BCT", 512 * s + 2 * s, 512 * s + 512, 4), view("ONE", 0, 128), [[0, 8], [-16, 16]], EQ, 0.0, 0, 1)
+    iota(full("OFI"), [[32, 14], [RW, 2]], 16, 0, False)
+    iota(view("WRI", 0, 32), [[128, 4], [-16, 8]], 112, 0, True)
+    for a in (0, 928):
+        iota(view("EW", a, a + 32), [[0, 32]], 0, 0, True)
+    for r in range(8):
+        iota(region(r, 464, RW), [[0, 16]], 0, 0, True)
+    on = view("ON", 0, 512)
+    iota(on, [[0, 512]], 1, 0, True)
+    pick(on, on, [[16, 8], [-1, 16], [0, 4]], EQ, 0.0, -112, 1)
+    for b in range(4):
+        pick(view("EBT", 512 * b, 512 * b + 512), on, [[0, 128], [1, 4]], EQ, 0.0, -b, 0)
 
-    def full(n):
-        return view(n, 0, 28)
-    ts(cb(5), pf(4), 0.0, None, EQ)
-    ts(cb(6), pf(4), 3.0, None, EQ)
-    ts(cb(9), pf(5), 32.0, None, MUL)
-    ts(full("GU"), full("DG"), pf(6), None, MUL)
-    tt(cb(7), cb(5), cb(6), ADD)
-    ts(cb(10), cb(5), -32.0, None, MUL)
-    tt(full("GI"), full("GU"), full("GE"), ADD)
-    tt(cb(8), pf(3), cb(7), SUB)
-    tt(cb(11), cb(9), cb(10), ADD)
-    ts(full("G1"), full("GI"), 1, None, AND)
     cp("V", full("MO"), full("MTI"))
-    tt(view("MW", 0, 448), (view("IN", 0, 448), full("MO")), view("IN2", 0, 448), SUB)
+    ts(full("OL"), full("OLI"), cb(0), None, SUB)
+    AW = view("AW", 0, C)
+    act(AW, (IN, full("OL")), bias=-224.0)
+    tt(view("SG0", 0, C), (IN, full("MO")), view("IN2", 0, C), GT)
+    cp("S", view("ND", 1, 896, 2), AW)
     quant("UQ", "US", 0, 128, "UT", 0)
-    ts(view("SG", 0, 448), view("MW", 0, 448), 0.0, 0.5, GT, SUB)
-    ts(view("SG", 448, 672), view("MW", 224, 448), 0.0, 0.5, AluOpType.is_le, SUB)
-    uq, us, uo = view("UQ", 0, 128), view("US", 0, 128), view("UO", 0, 8)
-    issue("V", lambda: g.vector.tensor_copy(T.URQ[:, 0:128].bitcast(dt.uint32), T.UQ[:, 0:128].bitcast(dt.uint32).indirect(T.UO[:, 0:8])), [uq, uo], [view("URQ", 0, 128)])
-    cp("V", view("URS", 0, 128), (us, uo))
-    quant("XQ", "XS", 0, 224, "X", 0)
-    quant("XQ", "XS", 224, 448, "X", 896)
-    tt(full("G2"), full("GI"), full("G1"), SUB)
-    ts(full("GV"), full("G1"), 16.0, cb(11), MUL, ADD)
-    ts(full("GC"), full("G2"), cb(8), None, EQ)
-    tt(full("GV"), full("GV"), full("ZBI"), ADD)
-    ts(full("GY"), full("GV"), 448.0, 448.0, MIN, SUB)
-    ts(full("GU"), full("GV"), 0.0, None, GE_)
-    tt(full("GY"), full("GY"), full("GC"), MUL)
-    tt(full("GU"), full("GY"), full("GU"), MUL)
-    ts(full("PL"), full("GU"), 448.0, None, ADD)
-
-    def tables():
-        ts(cb(2), pf(0), 240.0, None, SUB)
-        ts(cb(3), pf(1), 16.0, None, SUB)
-        ts(cb(4), pf(0), -0.0625, 1.0, MUL, ADD)
-        ts(cb(19), pf(0), -1.0, 16.0, MUL, ADD)
-        ii, n_, c_ = view("II", 0, 480), view("IN", 0, 480), cb(2)
-        issue("S", lambda: g.scalar.activation(ap(ii), ap(n_), IDENT, bias=ap(c_)), [n_, c_], [ii])
-        ts(view("E2", 0, 224), view("CCI", 0, 224), cb(3), None, ADD)
-        wq, wo = view("WQ", 0, 512), view("WRO", 0, 32)
-        ts(wo, view("WRI", 0, 32), pf(2), None, ADD)
-        issue("V", lambda: g.vector.tensor_copy(T.WRQ[:, 0:512].bitcast(dt.uint32), T.WQ[:, 0:512].bitcast(dt.uint32).indirect(T.WRO[:, 0:32])), [wq, wo], [view("WRQ", 0, 512)])
-        ts(view("OAB", 0, 30), view("MI", 224, 254), cb(19), None, ADD)
-        ts(view("OB", 0, 30), view("MI", 256, 286), cb(19), None, ADD)
-        ts(view("CC", 0, 224), view("E2", 0, 224), 0.0, 447.0, MAX, MIN)
-        cp("S", view("WAB0", 16, 480), (view("II", 0, 480), view("OAB", 0, 29)))
-        cp("S", region(R_WOWN, 0, 480), view("ZT", 0, 480))
-        for k in (R_M12, R_F34, R_P2, R_F56, R_P4, R_P1):
-            cp("S", region(k, 464, 480), view("ZT", 0, 16))
-        tt(view("DEL", 0, 224), view("MI", 0, 224), view("CC", 0, 224), SUB)
-        ts(view("CCB", 0, 224), view("CC", 0, 224), cb(19), None, ADD)
-        ts(view("DEL", 192, 224), view("DEL", 192, 224), cb(4), None, MUL)
-        ts(cb(1), pf(0), -31.0, 720.0, MUL, ADD)
-        fill(view("KV", 464, 512), 0.0)
+    pick_codes("URQ", "URS", "UQ", "US", 128, "UO", 8, "V")
+    tt(view("ND", 0, 896, 2), (AW, full("MO")), view("ND", 1, 896, 2), SUB)
+    act(view("SG", 0, C), view("SG0", 0, C), bias=-0.5)
+    for j in range(1, 7):
+        dma("Y", TAB, ND, "dtab", oap=T.TAB[j:128:16, :], iap=T.ND[16 * j:16 * j + 8, :], rows=True)
+    dma("Y", TAB, ND, "dtab", oap=T.TAB[ROW_A:128:32, :], iap=T.ND[0:4, :], rows=True)
+    dma("Y", TAB, ND, "dtab", oap=T.TAB[16 + ROW_B:128:32, :], iap=T.ND[112:116, :], rows=True)
+    cut = K["cut"]
+    runs = [(16 * a, 16 * e) for a, e in zip(cut, cut[1:])]
+    for a, e in runs:
+        quant("XQ", "XS", a, e, "X", 4 * a)
 
     def late(n):
-        if n == 1:
-            ts(cb(0), pf(0), -1.0, 240.0, MUL, ADD)
-            ts(cb(16), pf(3), 5.0, None, NE)
-            ts(cb(17), pf(0), -1.0, 496.0, MUL, ADD)
-            fill(view("OF", 28, 30), 480)
-            tt(cb(18), cb(17), cb(16), MUL)
-            ts(view("OF", 0, 28), view("CCI", 0, 28), pf(2), cb(18), ADD, ADD)
-        if n == 2:
-            ts(cb(12), pf(7), 96.0, None, GE_)
-            ts(cb(13), pf(7), 112.0, None, GE_)
-            tt(cb(14), cb(12), cb(13), SUB)
-        if n == 4:
-            ts(view("MK1", 0, 464), view("MD", 0, 464), cb(13), None, MAX)
-            ts(view("MK2", 0, 464), view("MD", 0, 464), cb(13), None, MUL)
-            for nm in ("WAB0", "WAB1"):
-                fill(view(nm, 0, 16), 0.0)
-                fill(view(nm, 480, 528), 0.0)
-        if n == 5:
-            cp("S", view("WRS", 0, 512), (view("WS", 0, 512), view("WRO", 0, 32)))
+        if n == 0:
+            ts(cb(1), pf(1), -1.0, 240.0, MUL, ADD)
+            ts(cb(2), pf(1), -1.0, 240.0 + RW * R_P, MUL, ADD)
+            ts(cb(3), pf(2), RW / 16.0, pf(0), MUL, ADD)
+            ts(view("WRO", 0, 32), view("WRI", 0, 32), pf(0), None, ADD)
+            ts(full("MO2"), full("MTI"), 2.0, 33.0, MUL, ADD)
+            ts(full("OF"), full("OFI"), cb(3), None, ADD)
 
-    def offsets(out, te, to, host, base, p0=0, p1=128):
-        ts(view(out, 0, 30, 2, p0, p1), view(te, 16 * host, 480, 32, p0, p1), base, None, ADD)
-        ts(view(out, 1, 30, 2, p0, p1), view(to, 16 * host, 480, 32, p0, p1), base, None, ADD)
-
-    def base_at(k, p0, p1):
-        return view("CB", k, k + 1, 1, p0, p1)
-
-    II = view("II", 0, 480)
     for r in range(3):
         peer = T.cores[rank ^ STEP[r]]
         n_in = len(topo.engines(peer, core))
-        arrives("RL%d" % r, 0, 28, "aL%d" % r, n_in)
-        for h in range(2):
-            count["aC%d%d" % (r, h)] = 2 * n_in
-            for nm in ("LQ%d" % r, "LS%d" % r):
-                log.setdefault(nm, []).append((access(view(nm, 224 * h, 224 * h + 224), True), True, "dma", ("aC%d%d" % (r, h), 2 * n_in, {})))
-        wab, wnew = "WAB%d" % (r % 2), "WAB%d" % ((r + 1) % 2)
-        for h in range(2):
-            mm(h, 224, "URQ", "URS", 0, "XQ", "XS", 224 * h)
-        for h in range(2):
-            tt(view("R", 224 * h, 224 * h + 224), view("PS", 512 * h, 512 * h + 224), view("SG", 224 * h, 224 * h + 224), MUL)
-        r2, rh = view("R2", 0, 224), view("R", 0, 224)
-        issue("S", lambda: g.scalar.activation(ap(r2), ap(rh), COPY, scale=-1.0), [rh], [r2])
-        tt(view("R2", 224, 448), view("PS", 512, 736), view("SG", 448, 672), MUL)
-        tt(view("DD", 0, 448), (view("R", 0, 448), full("MO")), view("R2", 0, 448), LT)
-        turn(view("TD", 0, 448), view("DD", 0, 448))
-        k = K["mt"]
-        cp("S", view("MT", 32 * k, 896, 2), (view("TD", 0, 464), view("PL", k, 28)))
-        cp("V", view("MT", 0, 32 * k, 2), (view("TD", 0, 464), view("PL", 0, k)))
+        arrives(["RL%d" % r], 0, 28, "aL%d" % r, n_in)
+        for h, (a, e) in enumerate(runs):
+            arrives(["LQ%d" % r, "LS%d" % r], a, e, "aC%d%d" % (r, h), n_in)
         if r == 0:
-            quant("BCQ", "BCS", 0, 128, "BCT", 0)
-        quant("MQ", "MS", 0, 224, "MT", 0)
-        mm(2, 224, "BCQ", "BCS", 0, "MQ", "MS", 0)
+            for h, (a, e) in enumerate(runs):
+                mm(4 + h, e - a, "URQ", "URS", 0, "XQ", "XS", a)
+            for s in range(2):
+                quant("BCQ", "BCS", 128 * s, 128 * s + 128, "BCT", 512 * s)
+        for h, (a, e) in enumerate(runs):
+            if r == 0 or h == len(runs) - 1:
+                tt(view("R", a, e), bank(4 + h, e - a), view("SG", a, e), MUL)
+                act(view("R2", a, e), view("R", a, e), scale=-1.0)
+        for h in range(2):
+            tt(view("MT", 512 * h, 512 * h + 448, 2), (view("R", 0, C), view("MO", 14 * h, 14 * h + 14)), view("R2", 224 * h, 224 * h + 224), LT)
+            quant("MQ", "MS", 128 * h, 128 * h + 128, "MT", 512 * h)
+            for s in range(2):
+                mm(2 * h + s, 128, "BCQ", "BCS", 128 * s, "MQ", "MS", 128 * h)
+                cp("S", view("FL", 448 * h + 2 * s + 1, 448 * h + 448, 4), bank(2 * h + s, 112))
         if r == 0:
-            tables()
-        parts = ((0, 64), (64, 224))
-        for a, b in parts:
-            tt(view("E1", a, b), view("PS", 1024 + a, 1024 + b), view("DEL", a, b), MUL)
-        tt(view("E2", 0, 64), view("E1", 0, 64), view("CCB", 0, 64), ADD)
-        cp("V", view("OE", 0, 64), view("E2", 0, 64))
-        tt(view("E2", 64, 224), view("E1", 64, 224), view("CCB", 64, 224), ADD)
-        split(("W1", 0), II, ("OE", 0), K["w1"])
-        gather("S", ("W23", 0), II, ("OE", 32))
-        dma("Y", region(R_WOWN, 0, 464)[:4] + (32, 64), view("W23", 0, 464, 1, 32, 64), "dwd")
-        cp("V", view("OE", 64, 224), view("E2", 64, 224))
-        split(("KA", 0), view("W1", 0, 464), ("OB", 0), K["ka"])
-        gather("S", ("MA", 0), view("W23", 0, 464), ("OAB", 0))
-        split(("KV", 0), view("KA", 0, 464), ("OE", 64), K["kv"])
-        gather("S", ("BIG", RW * R_M12), view("MA", 0, 464), ("OE", 96))
-        turn(view("TT1", 0, 480), view("KV", 0, 480))
-        turn(view("TT2", 0, 480), view("KV", 16, 496))
-        offsets("OK1", "TT1", "TT2", 0, cb(1))
-        w_in = {1: 0, 2: R_M12, 3: R_F34, 4: R_P3, 5: R_F56}
-        w_out = {1: R_P1, 2: R_P2, 3: R_P3, 4: R_P4, 5: R_P5}
-        for n in range(1, 6):
-            ok, host = "OK%d" % n, (n + 1) % 2
-            if n == 1:
-                split(("W45", 0), II, ("OE", 128), K["w45"])
-                dma("Y", region(R_WOWN, 0, 464)[:4] + (64, 80), view("W45", 0, 464, 1, 64, 80), "dwe")
-            split(("BIG", RW * w_out[n]), two(w_in[n]), (ok, 0), K["g1"][n - 1])
-            split(("KV", 16 * host), two(w_out[n] - 1 + host), (ok, 0), K["g2"][n - 1])
-            if n == 1:
-                gather("S", ("BIG", RW * R_F34), view("W45", 0, 464), ("OE", 32))
-            if n == 2:
-                gather("S", ("W6", 0), II, ("OE", 160))
-                dma("Y", region(R_WOWN, 0, 464)[:4] + (96, 112), view("W6", 0, 464, 1, 96, 112), "dwf")
-            if n == 3:
-                gather("S", ("BIG", RW * R_F56), view("W6", 0, 464), ("OE", 192))
-            if n == 4:
-                gather("S", (wnew, 16), view(wab, 16, 496), ("OE", 96))
-            if n == 5:
-                cp("S", region(R_WOWN, 0, 464)[:4] + (0, 32), view(wnew, 16, 480, 1, 0, 32))
-            turn(view("TT1", 0, 480), view("KV", 0, 480))
-            turn(view("TT2", 0, 480), view("KV", 16, 496))
-            if n < 5:
-                offsets("OK%d" % (n + 1), "TT1", "TT2", host, cb(1))
-            else:
-                offsets("OF", "TT1", "TT2", host, base_at(1, 96, 128), 96, 128)
-            if r == 0:
-                late(n)
-            if n == 1:
-                dma("Y", view("OF", 0, 28, 1, 32, 48), view("OK2", 1, 29, 1, 32, 48), "dk2")
-            if n == 2:
-                offsets("OK3B", "TT1", "TT2", host, 704.0)
-                dma("Y", view("OF", 0, 28, 1, 48, 64), view("OK3B", 0, 28, 1, 48, 64), "dk3")
-            if n == 3:
-                dma("Y", view("OF", 0, 28, 1, 64, 80), view("OK4", 1, 29, 1, 64, 80), "dk4")
-        gl = region(R_GL)
-        tt(gl, (two(R_P5), view("OF", 0, 29)), view("MK1", 0, 464), MUL)
-        tt(view("L7M", 0, 464), (two(R_GL), view("OF", 0, 29)), view("MK2", 0, 464), MUL)
-        rst = view("RST", 0, 464)
-
-        def scan(o, i):
-            issue("V", lambda: g.vector.tensor_tensor_scan(ap(o), ap(rst), ap(i), 0.0, MUL, ADD), [rst, i], [o])
-        scan(view("SC1", 0, 464), gl)
-        scan(view("SC2", 0, 464), view("L7M", 0, 464))
-        ts(view("U6", 0, 28, 1, 96, 128), view("SC1", 31, 464, 16, 96, 128), view("CB", 14, 15, 1, 96, 128), None, MUL)
-        cp("V", view("F", 0, 28, 1, 0, 96), view("SC1", 15, 448, 16, 0, 96))
-        tt(view("F", 0, 28, 1, 96, 128), view("SC2", 15, 448, 16, 96, 128), view("U6", 0, 28, 1, 96, 128), ADD)
-        for t in (2, 0, 3, 1):
-            ts(view("ZO", 28 * t, 28 * t + 28), full("F"), 4.0, float(896 + t), MUL, ADD)
-        ts(full("LST%d" % r), full("F"), 224.0, None, ADD)
-        send(peer, "RL%d" % r, "LST%d" % r, 0, 28, "aL%d" % r, False)
+            late(0)
+        for h in range(2):
+            o, f, t = view("EW", 32 + 448 * h, 480 + 448 * h), view("FL", 448 * h, 448 * h + 448), view("TAB", 448 * h, 448 * h + 448)
+            issue("V", lambda o=o, f=f, t=t: g.vector.tensor_tensor_scan(ap(o), ap(f), ap(t), 0.0, MUL, ADD), [f, t], [o])
+            turn(view("TA", 224 * h, 224 * h + 224), view("EW", 33 + 448 * h, 480 + 448 * h, 2))
+            turn(view("TB", 224 * h, 224 + 256 * h), view("EW", 1 + 448 * h, 448 + 512 * h, 2))
+        for off, row in (("OB", 16 + ROW_B), ("OA", ROW_A)):
+            ts(view(off, 0, 30, 2), view("TB", row, 480, 32), 2.0, 481.0, MUL, ADD)
+            ts(view(off, 1, 29, 2), view("TA", row, 448, 32), 2.0, 481.0, MUL, ADD)
+            if off == "OB":
+                cp("S", region(1, 16 * K["odd"], 464), (EW, view("OB", K["odd"], 29)))
+        cp("V", region(1, 0, 16 * K["odd"]), (EW, view("OB", 0, K["odd"])))
+        cp("S", region(0, 16 * K["even"], 464), (EW, view("OA", K["even"], 29)))
+        turn2("TT", "BIG", RW, RW, 16 * K["odd"])
+        ts(view("OK1", 0, 29), view("TT", 1, 464, 16), cb(1), None, ADD)
+        cp("V", region(0, 0, 16 * K["even"]), (EW, view("OA", 0, K["even"])))
+        for n in range(1, 7):
+            ok = "OK%d" % (n % 2)
+            split("BIG", RW * R_P, region(n - 1), ok, K["g1"])
+            if n < 6:
+                split("BIG", RW * (n + 1), region(R_P), ok, K["g2"])
+                if n < 5:
+                    cp("S", view("XP", C * (n - 1), C * n), view("X", n - 1, 1792, 4))
+                elif r < 2:
+                    cp("S", view("ND", 1, 896, 2), view("EW", 33, 928, 2))
+                turn2("TT", "BIG", RW * (n + 1), RW, 16 * K["g2"])
+                ts(view("OK%d" % ((n + 1) % 2), 0, 29), view("TT", n + 1, 464, 16), cb(1), None, ADD)
+                if n == 5:
+                    ts(view("OF", 1, 28, 2, 96, 128), view("TT", 16 + 6, 448, 32, 96, 128), view("CB", 2, 3, 1, 96, 128), None, ADD)
+        split("KV", 0, view("BIG", 0, RW * 8), "OF", K["last"], 28)
+        if r == 0:
+            cp("S", view("WRS", 0, 512), (view("WS", 0, 512), view("WRO", 0, 32)))
+        turn2("TT", "KV", 0, C, 16 * K["last"])
+        lst = "LST%d" % r
+        ts(full(lst), view("TT", ROW_L, C, 16), 224.0, None, ADD)
+        send(peer, "RL%d" % r, lst, 0, 28, "aL%d" % r, False)
+        if r == 0:
+            wq, wo = view("WQ", 0, 512), view("WRO", 0, 32)
+            issue("V", lambda: g.vector.tensor_copy(T.WRQ[:, 0:512].bitcast(dt.uint32), T.WQ[:, 0:512].bitcast(dt.uint32).indirect(T.WRO[:, 0:32])), [wq, wo], [view("WRQ", 0, 512)])
         for h in range(2):
             for t in range(4):
-                planes("Z", h, t, view("X", 0, 1792), "ZO", 28 * t, K["z"][h][t])
+                planes("Z", 14 * h, 14 * h + 14, t, view("XP", C * t, C * t + C), lst, K["z"][h][t])
             quant("ZQ", "ZS", 224 * h, 224 * h + 224, "Z", 896 * h)
             for b in range(4):
                 mm(4 * h + b, 224, "WRQ", "WRS", 128 * b, "ZQ", "ZS", 224 * h)
         for h in range(2):
             for b in range(4):
-                o, i = view("HP", 448 * b + 224 * h, 448 * b + 224 * h + 224), view("PS", 512 * (4 * h + b), 512 * (4 * h + b) + 224)
+                o, i = view("HP", C * b + 224 * h, C * b + 224 * h + 224), bank(4 * h + b, 224)
                 if (h, b) in K["hp"]:
                     ts(o, i, 0.03125, None, MUL)
                 else:
-                    issue("S", lambda o=o, i=i: g.scalar.activation(ap(o), ap(i), COPY, scale=0.03125), [i], [o])
-        for h in range(2):
+                    act(o, i, scale=0.03125)
+        for h, (a, e) in enumerate(runs):
             for b in range(4):
-                planes("HG", h, b, view("HP", 448 * b, 448 * b + 448), "RL%d" % r, 0, K["hg"][h][b])
-            quant("HQ%d" % r, "HS%d" % r, 224 * h, 224 * h + 224, "HG", 896 * h)
-            send(peer, "LQ%d" % r, "HQ%d" % r, 224 * h, 224 * h + 224, "aC%d%d" % (r, h), True)
-            send(peer, "LS%d" % r, "HS%d" % r, 224 * h, 224 * h + 224, "aC%d%d" % (r, h), False)
+                planes("HG", a // 16, e // 16, b, view("HP", C * b, C * b + C), "RL%d" % r, K["hg"][h][b])
+            quant("HQ%d" % r, "HS%d" % r, a, e, "HG", 4 * a)
+            send(peer, "LQ%d" % r, "HQ%d" % r, a, e, "aC%d%d" % (r, h), True)
+            send(peer, "LS%d" % r, "HS%d" % r, a, e, "aC%d%d" % (r, h), False)
         if r < 2:
-            turn(view("TT1", 0, 480), view(wnew, 0, 480))
-            turn(view("TT2", 0, 480), view(wnew, 16, 496))
-            turn(view("TT3", 0, 480), view(wnew, 32, 512))
-            offsets("OB", "TT1", "TT2", 1, cb(0))
-            offsets("OA", "TT2", "TT3", 0, cb(0))
-            offsets("OAB", "TT1", "TT2", 1, cb(0))
+            tt(view("ND", 0, 896, 2), (EW, full("MO2")), view("ND", 1, 896, 2), SUB)
             for k in range(4):
-                dma("Y", view("OAB", 0, 30, 1, 32 * k, 32 * k + 16), view("OA", 0, 30, 1, 32 * k, 32 * k + 16), "dmix")
+                for row, at in ((ROW_A, ROW_A), (112 + ROW_B, 16 + ROW_B)):
+                    dma("Y", TAB, ND, "dtab", oap=T.TAB[32 * k + at:32 * k + at + 1, :], iap=T.ND[row:row + 1, :], rows=True)
         else:
-            ts(full("LLO"), full("F"), cb(0), None, ADD)
-            lw, llo = view("LW", 0, 448), full("LLO")
-            issue("S", lambda: g.scalar.activation(ap(lw), ap(II).indirect(ap(llo)), IDENT, bias=224.0), [II, llo], [lw])
-            dma("Y", None, lw, "dout", oap=T.ll[:, :], iap=T.LW[0:128:16, :])
+            cp("S", view("LW", 0, C), (IN, full(lst)))
+            dma("Y", None, view("LW", 0, C), "dout", oap=T.ll[:, :], iap=T.LW[0:128:16, :])
             quant("VQ", "VS", 0, 128, "VT", 0)
         if r == 0:
             for b in range(4):
                 quant("EBQ", "EBS", 128 * b, 128 * b + 128, "EBT", 512 * b)
-        for h in range(2):
+        for h, (a, e) in enumerate(runs):
             for b in range(4):
-                mm(4 * h + b, 224, "EBQ", "EBS", 128 * b, "LQ%d" % r, "LS%d" % r, 224 * h)
+                mm(4 * (h % 2) + b, e - a, "EBQ", "EBS", 128 * b, "LQ%d" % r, "LS%d" % r, a)
             for b in range(4):
-                x = view("X", 896 * h + b, 896 * h + 896, 4)
-                tt(x, x, view("PS", 512 * (4 * h + b), 512 * (4 * h + b) + 224), ADD)
-            quant("XQ", "XS", 224 * h, 224 * h + 224, "X", 896 * h)
-    for h in range(2):
-        q, s = view("XQ", 224 * h, 224 * h + 224), view("XS", 224 * h, 224 * h + 224)
-        mm(h, 224, "VQ", "VS", 0, "XQ", "XS", 224 * h)
-        dma("Y", None, q, "dout", oap=T.oc[:, 896 * h:896 * h + 896], iap=T.XQ[:, 224 * h:224 * h + 224].bitcast(dt.uint8))
-        for k in range(4):
-            dma("Y", None, s, "dout", oap=T.osc[4 * k:4 * k + 4, 224 * h:224 * h + 224], iap=T.XS[32 * k:32 * k + 4, 224 * h:224 * h + 224])
-        y = view("YF", 224 * h, 224 * h + 224)
-        cp("VS"[h], y, view("PS", 512 * h, 512 * h + 224))
-        dma("Y" if h == 0 else "S", None, y, "dout", oap=T.y[:, 224 * h:224 * h + 224])
+                x = view("X", 4 * a + b, 4 * e, 4)
+                tt(x, x, bank(4 * (h % 2) + b, e - a), ADD)
+            quant("XQ", "XS", a, e, "X", 4 * a)
+            for j in ([h - 1] if h else []) + ([h] if h == len(runs) - 1 else []):
+                a2, e2 = runs[j]
+                if r < 2:
+                    mm(4 + j, e2 - a2, "URQ", "URS", 0, "XQ", "XS", a2)
+                    if j < len(runs) - 1:
+                        tt(view("R", a2, e2), bank(4 + j, e2 - a2), view("SG", a2, e2), MUL)
+                        act(view("R2", a2, e2), view("R", a2, e2), scale=-1.0)
+                else:
+                    mm(4 + j, e2 - a2, "VQ", "VS", 0, "XQ", "XS", a2)
+                    y = view("YF", a2, e2)
+                    cp("S", y, bank(4 + j, e2 - a2))
+                    dma("S", None, y, "dout", oap=T.y[:, a2:e2])
+            if r == 2:
+                dma("Y", None, view("XQ", a, e), "dout", oap=T.oc[:, 4 * a:4 * e], iap=T.XQ[:, a:e].bitcast(dt.uint8))
+    for k in range(4):
+        dma("Y", None, view("XS", 0, C), "dout", oap=T.osc[4 * k:4 * k + 4, :], iap=T.XS[32 * k:32 * k + 4, :])
     for s in sorted(count):
         if known["G"].get(s, 0) < count[s]:
             g.wait_ge(T.sem[s], int(count[s]))

import math
from concourse.mybir import dt, AluOpType, ActivationFunctionType

C, RW = 448, 480
ADD, SUB, MUL, MIN, MAX = AluOpType.add, AluOpType.subtract, AluOpType.mult, AluOpType.min, AluOpType.max
LT, GT, GE_, EQ, NE = AluOpType.is_lt, AluOpType.is_gt, AluOpType.is_ge, AluOpType.is_equal, AluOpType.not_equal
AND = AluOpType.bitwise_and
COPY, IDENT = ActivationFunctionType.Copy, ActivationFunctionType.Identity
STEP = [1, 2, 3]
ROW_A, ROW_B, ROW_L = 0, 7, 8
R_P = 7
K = {"g1": 14, "g2": 12, "odd": 14, "even": 8, "last": 12, "cut": [0, 14, 28],
     "hp": [(0, 0), (0, 1), (1, 0), (1, 1)], "z": [[14, 12, 0, 0], [14, 8, 0, 0]], "hg": [[14, 14, 6, 0], [14, 6, 0, 0]]}

SCRATCH = {
    "X": ("sbuf", [128, 1792], "bfloat16"), "XP": ("sbuf", [128, 1792], "bfloat16"),
    "UT": ("sbuf", [128, 512], "bfloat16"), "VT": ("sbuf", [128, 512], "bfloat16"),
    "XQ": ("sbuf", [128, 448], "float8_e4m3fn_x4"), "XS": ("sbuf", [128, 448], "uint8"),
    "UQ": ("sbuf", [128, 128], "float8_e4m3fn_x4"), "US": ("sbuf", [128, 128], "uint8"),
    "URQ": ("sbuf", [128, 128], "float8_e4m3fn_x4"), "URS": ("sbuf", [128, 128], "uint8"),
    "VQ": ("sbuf", [128, 128], "float8_e4m3fn_x4"), "VS": ("sbuf", [128, 128], "uint8"),
    "WQ": ("sbuf", [128, 512], "float8_e4m3fn_x4"), "WS": ("sbuf", [128, 512], "uint8"),
    "WRQ": ("sbuf", [128, 512], "float8_e4m3fn_x4"), "WRS": ("sbuf", [128, 512], "uint8"),
    "WRI": ("sbuf", [128, 32], "float32"), "WRO": ("sbuf", [128, 32], "uint16"),
    "BCT": ("sbuf", [128, 1024], "bfloat16"), "BCQ": ("sbuf", [128, 256], "float8_e4m3fn_x4"), "BCS": ("sbuf", [128, 256], "uint8"),
    "ON": ("sbuf", [128, 512], "bfloat16"), "ONE": ("sbuf", [128, 128], "bfloat16"), "EBT": ("sbuf", [128, 2048], "bfloat16"),
    "EBQ": ("sbuf", [128, 512], "float8_e4m3fn_x4"), "EBS": ("sbuf", [128, 512], "uint8"),
    "PS": ("psum", [128, 4096], "float32"),
    "MTI": ("sbuf", [128, 28], "int32"), "MO": ("sbuf", [128, 28], "uint16"), "MO2": ("sbuf", [128, 28], "uint16"),
    "OLI": ("sbuf", [128, 28], "int32"), "OL": ("sbuf", [128, 28], "uint16"),
    "IN": ("sbuf", [128, 448], "float32"), "IN2": ("sbuf", [128, 448], "float32"), "SG": ("sbuf", [128, 448], "bfloat16"), "SG0": ("sbuf", [128, 448], "bfloat16"),
    "AW": ("sbuf", [128, 448], "bfloat16"), "ND": ("sbuf", [128, 896], "float16"), "TAB": ("sbuf", [128, 896], "float16"),
    "FL": ("sbuf", [128, 896], "bfloat16"), "EW": ("sbuf", [128, 960], "bfloat16"),
    "PI": ("sbuf", [128, 1], "int32"), "PC": ("sbuf", [128, 4], "int32"), "PF": ("sbuf", [128, 4], "float32"), "CB": ("sbuf", [128, 8], "float32"),
    "URI": ("sbuf", [128, 8], "int32"), "UO": ("sbuf", [128, 8], "uint16"), "OFI": ("sbuf", [128, 28], "int32"),
    "R": ("sbuf", [128, 448], "float32"), "R2": ("sbuf", [128, 448], "float32"),
    "MT": ("sbuf", [128, 1024], "bfloat16"), "MQ": ("sbuf", [128, 256], "float8_e4m3fn_x4"), "MS": ("sbuf", [128, 256], "uint8"),
    "BIG": ("sbuf", [128, RW * 8], "bfloat16"), "KV": ("sbuf", [128, 448], "bfloat16"),
    "TT": ("sbuf", [128, 480], "bfloat16"), "TA": ("sbuf", [128, 448], "bfloat16"), "TB": ("sbuf", [128, 480], "bfloat16"),
    "OA": ("sbuf", [128, 30], "uint16"), "OB": ("sbuf", [128, 30], "uint16"), "OF": ("sbuf", [128, 28], "uint16"),
    "OK0": ("sbuf", [128, 30], "uint16"), "OK1": ("sbuf", [128, 30], "uint16"),
    "Z": ("sbuf", [128, 1792], "bfloat16"), "ZQ": ("sbuf", [128, 448], "float8_e4m3fn_x4"), "ZS": ("sbuf", [128, 448], "uint8"),
    "HP": ("sbuf", [128, 1792], "bfloat16"), "HG": ("sbuf", [128, 1792], "bfloat16"),
    "LW": ("sbuf", [128, 448], "float32"), "YF": ("sbuf", [128, 448], "float32"),
}
for _n in range(3):
    SCRATCH["HQ%d" % _n] = ("sbuf", [128, 448], "float8_e4m3fn_x4")
    SCRATCH["HS%d" % _n] = ("sbuf", [128, 448], "uint8")
    SCRATCH["LQ%d" % _n] = ("sbuf", [128, 448], "float8_e4m3fn_x4")
    SCRATCH["LS%d" % _n] = ("sbuf", [128, 448], "uint8")
    SCRATCH["LST%d" % _n] = ("sbuf", [128, 28], "uint16")
    SCRATCH["RL%d" % _n] = ("sbuf", [128, 28], "uint16")
SEMAPHORES = ["qV", "qS", "qP", "qG", "dx0", "dx1", "du", "dm", "dl", "dw", "dv", "dtab", "dout", "lsend"]
SEMAPHORES += ["aL%d" % _n for _n in range(3)] + ["aC%d%d" % (_n, _h) for _n in range(3) for _h in range(3)]
PSUM_BANK = 512


def rank_program(g, core, T, topo):
    rank = T.rank_of(core)
    if rank is None:
        return
    Q = {"V": g.vector, "S": g.scalar, "P": g.tensor, "G": g, "Y": g.sync}
    known = {q: {} for q in Q}
    count, log = {}, {}

    def view(name, c0, c1, step=1, p0=0, p1=128):
        return (name, c0, c1, step, p0, p1)

    def ap(v):
        n, c0, c1, step, p0, p1 = v
        return T[n][p0:p1, c0:c1] if step == 1 else T[n][p0:p1, c0:c1:step]

    def access(v, w):
        n, c0, c1, step, p0, p1 = v
        if n == "PS":
            return (n, c0 // PSUM_BANK, (c1 - 1) // PSUM_BANK + 1, 1, 0, 128, True)
        return (n, c0, c1, step, p0, p1, w)

    def hit(a, b):
        if a[4] >= b[5] or b[4] >= a[5] or a[1] >= b[2] or b[1] >= a[2]:
            return False
        k = math.gcd(a[3], b[3])
        return k == 1 or (a[1] - b[1]) % k == 0

    def issue(q, fn, reads, writes, sem=None, inc=16, chain=True, rows=False):
        accs = [(access(v, False), False) for v in reads] + [(access(v, True), True) for v in writes]
        need = []
        for a, w in accs:
            for (b, bw, bq, tok) in log.get(a[0], []):
                if not (a[6] or b[6]) or not hit(a, b):
                    continue
                if bq == q and sem is None and not bw:
                    continue
                s, n, snap = tok
                if rows and s == sem:
                    continue
                if bq == "dma":
                    n = count[s]
                need.append((s, n, snap))
        need.sort(key=lambda e: -len(e[2]))
        for s, n, snap in sorted(need, key=lambda e: (-e[1] if e[0] in ("qV", "qS", "qP", "qG") else 0)):
            if known[q].get(s, 0) >= n:
                continue
            Q[q].wait_ge(T.sem[s], int(n))
            for k2, v2 in snap.items():
                known[q][k2] = max(known[q].get(k2, 0), v2)
            known[q][s] = n
        inst = fn()
        name = sem if sem is not None else "q" + q
        count[name] = count.get(name, 0) + (inc if sem is not None else 1)
        if chain:
            inst.then_inc(T.sem[name], inc if sem is not None else 1)
        tok = (name, count[name], dict(known[q]))
        for a, w in accs:
            lst = log.setdefault(a[0], [])
            if w or a[0] == "PS":
                if a[3] == 1 and not rows:
                    lst[:] = [e for e in lst if not (a[1] <= e[0][1] and e[0][2] <= a[2] and a[4] <= e[0][4] and e[0][5] <= a[5])]
            else:
                lst[:] = [e for e in lst if not (e[0] == a and e[2] == q and q != "Y" and sem is None and not e[1])]
            lst.append((a, w, "dma" if sem is not None else q, tok))

    def sc(v):
        return ap(v) if isinstance(v, tuple) else v

    def src(a):
        if len(a) == 2:
            return ap(a[0]).indirect(ap(a[1])), [a[0], a[1]]
        return ap(a), [a]

    def ts(out, in0, s1, s2=None, op0=ADD, op1=None):
        e, rd = src(in0)
        rd = rd + [s for s in (s1, s2) if isinstance(s, tuple)]
        if op1 is None:
            issue("V", lambda: g.vector.tensor_scalar(ap(out), e, sc(s1), None, op0), rd, [out])
        else:
            issue("V", lambda: g.vector.tensor_scalar(ap(out), e, sc(s1), sc(s2), op0, op1), rd, [out])

    def tt(out, in0, in1, op):
        e, rd = src(in0)
        issue("V", lambda: g.vector.tensor_tensor(ap(out), e, ap(in1), op), rd + [in1], [out])

    def cp(q, out, in_):
        e, rd = src(in_)
        if q == "V":
            issue("V", lambda: g.vector.tensor_copy(ap(out), e), rd, [out])
        else:
            issue("S", lambda: g.scalar.activation(ap(out), e, COPY), rd, [out])

    def act(out, in_, scale=1.0, bias=0.0):
        e, rd = src(in_)
        issue("S", lambda: g.scalar.activation(ap(out), e, IDENT if bias else COPY, bias=bias, scale=scale), rd, [out])

    def fill(out, k):
        issue("V", lambda: g.vector.memset(ap(out), k), [], [out])

    def turn(out, in_):
        issue("V", lambda: g.vector.transpose(ap(out), ap(in_)), [in_], [out])

    def quant(q, s, c0, c1, t, e0):
        o, p, i = view(q, c0, c1), view(s, c0, c1), view(t, e0, e0 + 4 * (c1 - c0))
        issue("V", lambda: g.vector.quantize_mx(ap(o), ap(p), ap(i)), [i], [o, p])

    def bank(b, n):
        return view("PS", PSUM_BANK * b, PSUM_BANK * b + n)

    def mm(b, n, wq, ws, w0, xq, xs, x0):
        o = bank(b, n)
        a, e, c, d = view(wq, w0, w0 + 128), view(ws, w0, w0 + 128), view(xq, x0, x0 + n), view(xs, x0, x0 + n)
        issue("P", lambda: g.tensor.matmul_mx(ap(o), ap(a), ap(e), ap(c), ap(d), True, True), [a, e, c, d], [o])

    def dma(q, out, in_, sem, oap=None, iap=None, rows=False):
        o = oap if oap is not None else ap(out)
        i = iap if iap is not None else ap(in_)
        issue(q, lambda: Q[q].dma_start(o, i), [in_] if in_ is not None else [], [out] if out is not None else [], sem=sem, rows=rows)

    def send(dst, oname, iname, c0, c1, rsem, codes):
        rid, pid, _s = topo.addr(dst)
        i, o = T[iname][:, c0:c1], T[oname][:, c0:c1]
        if codes:
            i, o = i.bitcast(dt.uint8), o.bitcast(dt.uint8)
        n = len(topo.engines(core, dst))
        issue("G", lambda: g.remote_dma(o, i, T.sem[rsem], T.sem["lsend"], pid, rid, topo.mask(core, dst)), [view(iname, c0, c1)], [], sem="lsend", inc=n, chain=False)

    def arrives(names, c0, c1, sem, n):
        count[sem] = n * len(names)
        for name in names:
            log.setdefault(name, []).append((access(view(name, c0, c1), True), True, "dma", (sem, count[sem], {})))

    def iota(out, pattern, base, ch, flag):
        if flag:
            issue("G", lambda: g.iota(ap(out), pattern, base, ch, allow_small_or_imprecise_dtypes=True), [], [out])
        else:
            issue("G", lambda: g.iota(ap(out), pattern, base, ch), [], [out])

    def pick(out, in_, pattern, op, fill_, base, ch):
        issue("G", lambda: g.affine_select(ap(out), ap(in_), pattern, op, fill_, base, ch), [in_], [out])

    def pick_codes(oq, os_, q, s, n, off, k, sq):
        o, i, f = view(oq, 0, 16 * k), view(q, 0, n), view(off, 0, k)
        issue("V", lambda: g.vector.tensor_copy(ap(o).bitcast(dt.uint32), ap(i).bitcast(dt.uint32).indirect(ap(f))), [i, f], [o])
        cp(sq, view(os_, 0, 16 * k), (view(s, 0, n), f))

    def pf(k):
        return view("PF", k, k + 1)

    def cb(k):
        return view("CB", k, k + 1)

    def full(n):
        return view(n, 0, 28)

    def region(r, a=0, b=RW):
        return view("BIG", RW * r + a, RW * r + b)

    def split(out, o0, win, off, k, n=29):
        if k < n:
            cp("S", view(out, o0 + 16 * k, o0 + 16 * n), (win, view(off, k, n)))
        if k > 0:
            cp("V", view(out, o0, o0 + 16 * k), (win, view(off, 0, k)))

    def turn2(out, name, c0, n, k):
        turn(view(out, 0, k), view(name, c0, c0 + k))
        turn(view(out, k, n), view(name, c0 + k, c0 + n))

    def planes(out, a, e, b, win, off, k):
        if k > 0:
            cp("V", view(out, 64 * a + b, 64 * (a + k), 4), (win, view(off, a, a + k)))
        if a + k < e:
            cp("S", view(out, 64 * (a + k) + b, 64 * e, 4), (win, view(off, a + k, e)))

    IN, EW, TAB, ND = view("IN", 0, C), view("EW", 0, 960), view("TAB", 0, 896), view("ND", 0, 896)
    iota(full("OLI"), [[16, 28]], 0, 1, False)
    iota(view("PI", 0, 1), [[0, 1]], 0, 1, False)
    iota(view("URI", 0, 8), [[16, 8]], 0, 0, False)
    iota(IN, [[1, C]], 0, 0, True)
    dma("Y", full("MTI"), None, "dm", iap=T.mt[:, :])
    dma("S", view("X", 896, 1792), None, "dx1", iap=T.x[:, 896:1792])
    dma("Y", view("X", 0, 896), None, "dx0", iap=T.x[:, 0:896])
    dma("S", view("UT", 0, 512), None, "du", iap=T.u[:, :])
    dma("Y", view("OLI", 0, 28, 1, 0, 16), None, "dl", iap=T.la[:, :])
    dma("S", view("OLI", 0, 28, 1, 112, 128), None, "dl", iap=T.lb[:, :])
    dma("Y", view("WQ", 0, 512), None, "dw", oap=T.WQ[:, 0:512].bitcast(dt.uint8), iap=T.wc[:, :])
    dma("Y", view("WS", 0, 512), None, "dw", iap=T.ws[:, :])
    dma("Y", view("VT", 0, 512), None, "dv", iap=T.v[:, :])

    fill(view("ONE", 0, 128), 1.0)
    fill(view("BCT", 0, 1024), 0.0)
    p = view("PI", 0, 1)
    for k, m in enumerate((15, 16, 96, 112)):
        ts(view("PC", k, k + 1), p, m, None, AND)
    fill(view("TAB", 0, 896, 2), 0.0)
    cp("V", view("PF", 0, 4), view("PC", 0, 4))
    ts(view("UO", 0, 8), view("URI", 0, 8), 0.0, None, ADD)
    fill(view("FL", 0, 896, 2), 0.0)
    ts(cb(0), pf(3), 112.0, pf(3), NE, MUL)
    fill(view("MT", 0, 1024), 0.0)
    cp("S", view("IN2", 0, C), IN)
    act(view("TAB", 1, 896, 2), IN, bias=-224.0)
    for s in range(2):
        pick(view("BCT", 512 * s + 2 * s, 512 * s + 512, 4), view("ONE", 0, 128), [[0, 8], [-16, 16]], EQ, 0.0, 0, 1)
    iota(full("OFI"), [[32, 14], [RW, 2]], 16, 0, False)
    iota(view("WRI", 0, 32), [[128, 4], [-16, 8]], 112, 0, True)
    for a in (0, 928):
        iota(view("EW", a, a + 32), [[0, 32]], 0, 0, True)
    for r in range(8):
        iota(region(r, 464, RW), [[0, 16]], 0, 0, True)
    on = view("ON", 0, 512)
    iota(on, [[0, 512]], 1, 0, True)
    pick(on, on, [[16, 8], [-1, 16], [0, 4]], EQ, 0.0, -112, 1)
    for b in range(4):
        pick(view("EBT", 512 * b, 512 * b + 512), on, [[0, 128], [1, 4]], EQ, 0.0, -b, 0)

    cp("V", full("MO"), full("MTI"))
    ts(full("OL"), full("OLI"), cb(0), None, SUB)
    AW = view("AW", 0, C)
    act(AW, (IN, full("OL")), bias=-224.0)
    tt(view("SG0", 0, C), (IN, full("MO")), view("IN2", 0, C), GT)
    cp("S", view("ND", 1, 896, 2), AW)
    quant("UQ", "US", 0, 128, "UT", 0)
    pick_codes("URQ", "URS", "UQ", "US", 128, "UO", 8, "V")
    tt(view("ND", 0, 896, 2), (AW, full("MO")), view("ND", 1, 896, 2), SUB)
    act(view("SG", 0, C), view("SG0", 0, C), bias=-0.5)
    for j in range(1, 7):
        dma("Y", TAB, ND, "dtab", oap=T.TAB[j:128:16, :], iap=T.ND[16 * j:16 * j + 8, :], rows=True)
    dma("Y", TAB, ND, "dtab", oap=T.TAB[ROW_A:128:32, :], iap=T.ND[0:4, :], rows=True)
    dma("Y", TAB, ND, "dtab", oap=T.TAB[16 + ROW_B:128:32, :], iap=T.ND[112:116, :], rows=True)
    cut = K["cut"]
    runs = [(16 * a, 16 * e) for a, e in zip(cut, cut[1:])]
    for a, e in runs:
        quant("XQ", "XS", a, e, "X", 4 * a)

    def late(n):
        if n == 0:
            ts(cb(1), pf(1), -1.0, 240.0, MUL, ADD)
            ts(cb(2), pf(1), -1.0, 240.0 + RW * R_P, MUL, ADD)
            ts(cb(3), pf(2), RW / 16.0, pf(0), MUL, ADD)
            ts(view("WRO", 0, 32), view("WRI", 0, 32), pf(0), None, ADD)
            ts(full("MO2"), full("MTI"), 2.0, 33.0, MUL, ADD)
            ts(full("OF"), full("OFI"), cb(3), None, ADD)

    for r in range(3):
        peer = T.cores[rank ^ STEP[r]]
        n_in = len(topo.engines(peer, core))
        arrives(["RL%d" % r], 0, 28, "aL%d" % r, n_in)
        for h, (a, e) in enumerate(runs):
            arrives(["LQ%d" % r, "LS%d" % r], a, e, "aC%d%d" % (r, h), n_in)
        if r == 0:
            for h, (a, e) in enumerate(runs):
                mm(4 + h, e - a, "URQ", "URS", 0, "XQ", "XS", a)
            for s in range(2):
                quant("BCQ", "BCS", 128 * s, 128 * s + 128, "BCT", 512 * s)
        for h, (a, e) in enumerate(runs):
            if r == 0 or h == len(runs) - 1:
                tt(view("R", a, e), bank(4 + h, e - a), view("SG", a, e), MUL)
                act(view("R2", a, e), view("R", a, e), scale=-1.0)
        for h in range(2):
            tt(view("MT", 512 * h, 512 * h + 448, 2), (view("R", 0, C), view("MO", 14 * h, 14 * h + 14)), view("R2", 224 * h, 224 * h + 224), LT)
            quant("MQ", "MS", 128 * h, 128 * h + 128, "MT", 512 * h)
            for s in range(2):
                mm(2 * h + s, 128, "BCQ", "BCS", 128 * s, "MQ", "MS", 128 * h)
                cp("S", view("FL", 448 * h + 2 * s + 1, 448 * h + 448, 4), bank(2 * h + s, 112))
        if r == 0:
            late(0)
        for h in range(2):
            o, f, t = view("EW", 32 + 448 * h, 480 + 448 * h), view("FL", 448 * h, 448 * h + 448), view("TAB", 448 * h, 448 * h + 448)
            issue("V", lambda o=o, f=f, t=t: g.vector.tensor_tensor_scan(ap(o), ap(f), ap(t), 0.0, MUL, ADD), [f, t], [o])
            turn(view("TA", 224 * h, 224 * h + 224), view("EW", 33 + 448 * h, 480 + 448 * h, 2))
            turn(view("TB", 224 * h, 224 + 256 * h), view("EW", 1 + 448 * h, 448 + 512 * h, 2))
        for off, row in (("OB", 16 + ROW_B), ("OA", ROW_A)):
            ts(view(off, 0, 30, 2), view("TB", row, 480, 32), 2.0, 481.0, MUL, ADD)
            ts(view(off, 1, 29, 2), view("TA", row, 448, 32), 2.0, 481.0, MUL, ADD)
            if off == "OB":
                cp("S", region(1, 16 * K["odd"], 464), (EW, view("OB", K["odd"], 29)))
        cp("V", region(1, 0, 16 * K["odd"]), (EW, view("OB", 0, K["odd"])))
        cp("S", region(0, 16 * K["even"], 464), (EW, view("OA", K["even"], 29)))
        turn2("TT", "BIG", RW, RW, 16 * K["odd"])
        ts(view("OK1", 0, 29), view("TT", 1, 464, 16), cb(1), None, ADD)
        cp("V", region(0, 0, 16 * K["even"]), (EW, view("OA", 0, K["even"])))
        for n in range(1, 7):
            ok = "OK%d" % (n % 2)
            split("BIG", RW * R_P, region(n - 1), ok, K["g1"])
            if n < 6:
                split("BIG", RW * (n + 1), region(R_P), ok, K["g2"])
                if n < 5:
                    cp("S", view("XP", C * (n - 1), C * n), view("X", n - 1, 1792, 4))
                elif r < 2:
                    cp("S", view("ND", 1, 896, 2), view("EW", 33, 928, 2))
                turn2("TT", "BIG", RW * (n + 1), RW, 16 * K["g2"])
                ts(view("OK%d" % ((n + 1) % 2), 0, 29), view("TT", n + 1, 464, 16), cb(1), None, ADD)
                if n == 5:
                    ts(view("OF", 1, 28, 2, 96, 128), view("TT", 16 + 6, 448, 32, 96, 128), view("CB", 2, 3, 1, 96, 128), None, ADD)
        split("KV", 0, view("BIG", 0, RW * 8), "OF", K["last"], 28)
        if r == 0:
            cp("S", view("WRS", 0, 512), (view("WS", 0, 512), view("WRO", 0, 32)))
        turn2("TT", "KV", 0, C, 16 * K["last"])
        lst = "LST%d" % r
        ts(full(lst), view("TT", ROW_L, C, 16), 224.0, None, ADD)
        send(peer, "RL%d" % r, lst, 0, 28, "aL%d" % r, False)
        if r == 0:
            wq, wo = view("WQ", 0, 512), view("WRO", 0, 32)
            issue("V", lambda: g.vector.tensor_copy(T.WRQ[:, 0:512].bitcast(dt.uint32), T.WQ[:, 0:512].bitcast(dt.uint32).indirect(T.WRO[:, 0:32])), [wq, wo], [view("WRQ", 0, 512)])
        for h in range(2):
            for t in range(4):
                planes("Z", 14 * h, 14 * h + 14, t, view("XP", C * t, C * t + C), lst, K["z"][h][t])
            quant("ZQ", "ZS", 224 * h, 224 * h + 224, "Z", 896 * h)
            for b in range(4):
                mm(4 * h + b, 224, "WRQ", "WRS", 128 * b, "ZQ", "ZS", 224 * h)
        for h in range(2):
            for b in range(4):
                o, i = view("HP", C * b + 224 * h, C * b + 224 * h + 224), bank(4 * h + b, 224)
                if (h, b) in K["hp"]:
                    ts(o, i, 0.03125, None, MUL)
                else:
                    act(o, i, scale=0.03125)
        for h, (a, e) in enumerate(runs):
            for b in range(4):
                planes("HG", a // 16, e // 16, b, view("HP", C * b, C * b + C), "RL%d" % r, K["hg"][h][b])
            quant("HQ%d" % r, "HS%d" % r, a, e, "HG", 4 * a)
            send(peer, "LQ%d" % r, "HQ%d" % r, a, e, "aC%d%d" % (r, h), True)
            send(peer, "LS%d" % r, "HS%d" % r, a, e, "aC%d%d" % (r, h), False)
        if r < 2:
            tt(view("ND", 0, 896, 2), (EW, full("MO2")), view("ND", 1, 896, 2), SUB)
            for k in range(4):
                for row, at in ((ROW_A, ROW_A), (112 + ROW_B, 16 + ROW_B)):
                    dma("Y", TAB, ND, "dtab", oap=T.TAB[32 * k + at:32 * k + at + 1, :], iap=T.ND[row:row + 1, :], rows=True)
        else:
            cp("S", view("LW", 0, C), (IN, full(lst)))
            dma("Y", None, view("LW", 0, C), "dout", oap=T.ll[:, :], iap=T.LW[0:128:16, :])
            quant("VQ", "VS", 0, 128, "VT", 0)
        if r == 0:
            for b in range(4):
                quant("EBQ", "EBS", 128 * b, 128 * b + 128, "EBT", 512 * b)
        for h, (a, e) in enumerate(runs):
            for b in range(4):
                mm(4 * (h % 2) + b, e - a, "EBQ", "EBS", 128 * b, "LQ%d" % r, "LS%d" % r, a)
            for b in range(4):
                x = view("X", 4 * a + b, 4 * e, 4)
                tt(x, x, bank(4 * (h % 2) + b, e - a), ADD)
            quant("XQ", "XS", a, e, "X", 4 * a)
            for j in ([h - 1] if h else []) + ([h] if h == len(runs) - 1 else []):
                a2, e2 = runs[j]
                if r < 2:
                    mm(4 + j, e2 - a2, "URQ", "URS", 0, "XQ", "XS", a2)
                    if j < len(runs) - 1:
                        tt(view("R", a2, e2), bank(4 + j, e2 - a2), view("SG", a2, e2), MUL)
                        act(view("R2", a2, e2), view("R", a2, e2), scale=-1.0)
                else:
                    mm(4 + j, e2 - a2, "VQ", "VS", 0, "XQ", "XS", a2)
                    y = view("YF", a2, e2)
                    cp("S", y, bank(4 + j, e2 - a2))
                    dma("S", None, y, "dout", oap=T.y[:, a2:e2])
            if r == 2:
                dma("Y", None, view("XQ", a, e), "dout", oap=T.oc[:, 4 * a:4 * e], iap=T.XQ[:, a:e].bitcast(dt.uint8))
    for k in range(4):
        dma("Y", None, view("XS", 0, C), "dout", oap=T.osc[4 * k:4 * k + 4, :], iap=T.XS[32 * k:32 * k + 4, :])
    for s in sorted(count):
        if known["G"].get(s, 0) < count[s]:
            g.wait_ge(T.sem[s], int(count[s]))
